import numpy as np
import ml_dtypes


def mxq(x, axis, fmt="e4m3"):
    dtype, down = {"e4m3": (ml_dtypes.float8_e4m3fn, 7), "e5m2": (ml_dtypes.float8_e5m2, 14)}[fmt]
    v = np.moveaxis(np.asarray(x, np.float32).astype(ml_dtypes.bfloat16).astype(np.float64), axis, -1)
    blocks = v.reshape(v.shape[:-1] + (-1, 32))
    amax = np.abs(blocks).max(-1, keepdims=True)
    byte = np.maximum(np.where(amax > 0, np.frexp(amax)[1] - 1 + 127, 0) - down, 1)
    scale = np.exp2(byte - 127.0)
    codes = (blocks / scale).astype(np.float32).astype(dtype).astype(np.float64)
    return np.moveaxis((codes * scale).reshape(v.shape), -1, axis)


WIDE = False


def mx_kscale(k):
    if not WIDE:
        return np.ones(k)
    levels = np.array([10, -10, 5, -5, 0])
    if k % 512:
        return np.exp2(np.random.permutation(np.resize(levels, k // 32))).repeat(32)
    a = np.empty((k // 512, 16))
    for p in range(k // 512):
        a[p, :8] = np.random.permutation(np.resize(levels, 8))
        for g in range(8):
            far = levels[np.abs(levels - a[p, g]) >= 10]
            a[p, g + 8] = far[np.random.randint(len(far))]
    return np.exp2(a.ravel()).repeat(32)


BF16 = ml_dtypes.bfloat16


def bf(x):
    return np.asarray(x, np.float32).astype(BF16)


def f64(x):
    return np.asarray(x).astype(np.float64)


E2M1 = np.array([0.0, 0.5, 1.0, 1.5, 2.0, 3.0, 4.0, 6.0, -0.0, -0.5, -1.0, -1.5, -2.0, -3.0, -4.0, -6.0])


def pack_weight(w, fmt):
    k, n = w.shape
    w = f64(bf(w)).reshape(k // 32, 32, n)
    amax = np.abs(w).max(1)
    if fmt == "e4m3":
        byte = np.frexp(amax)[1] - 1 + 127 - 7
    else:
        mant, ex = np.frexp(amax / 6.0)
        byte = np.where(mant > 0.5, ex, ex - 1) + 127
    byte = np.clip(np.where(amax > 0, byte, 1), 1, 254)
    scaled = (w * np.exp2(127.0 - byte)[:, None, :]).reshape(k, n).astype(np.float32)
    by_word = np.ascontiguousarray(scaled.reshape(k // 512, 128, 4, n).transpose(0, 1, 3, 2))
    if fmt == "e4m3":
        words = by_word.astype(ml_dtypes.float8_e4m3fn).view(np.uint8)
    else:
        c = by_word.astype(ml_dtypes.float4_e2m1fn).view(np.uint8) & 0xF
        words = c[..., 0::2] | (c[..., 1::2] << 4)
    return np.ascontiguousarray(words), np.ascontiguousarray(byte.astype(np.uint8).reshape(k // 512, 16, n))


def unpack_weight(words, scales, fmt):
    g, p, n, _ = words.shape
    if fmt == "e4m3":
        vals = np.ascontiguousarray(words).view(ml_dtypes.float8_e4m3fn).astype(np.float64)
    else:
        nib = np.empty((g, p, n, 4), np.uint8)
        nib[..., 0::2] = words & 0xF
        nib[..., 1::2] = words >> 4
        vals = E2M1[nib]
    vals = vals * np.repeat(np.exp2(scales.astype(np.float64) - 127.0), 8, axis=1)[..., None]
    return vals.transpose(0, 1, 3, 2).reshape(g * 512, n)
def pack4(w):
    words, scales = pack_weight(w, "e2m1")
    return words.reshape(words.shape[0], 128, -1), scales


def unpack4(words, scales):
    return unpack_weight(words.reshape(words.shape[0], 128, -1, 2), scales, "e2m1")


def planes(Y):
    n, m = Y.shape
    b = f64(bf(Y)).reshape(n // 32, 32, m)
    amax = np.abs(b).max(1)
    byte = np.clip(np.where(amax > 0, np.frexp(amax)[1] - 1 + 127 - 7, 1), 1, 254)
    codes = (b * np.exp2(127.0 - byte)[:, None, :]).reshape(n, m).astype(np.float32).astype(ml_dtypes.float8_e4m3fn).view(np.uint8)
    words = codes.reshape(n // 512, 128, 4, m).transpose(0, 1, 3, 2)
    return np.ascontiguousarray(words), np.ascontiguousarray(byte.astype(np.uint8).reshape(n // 512, 16, m))


N, D, F = 2048, 512, 1024


def setup_inputs():
    s, t = mx_kscale(D), mx_kscale(N)
    x = np.random.standard_normal((N, D)) * s[None, :]
    f = np.random.standard_normal((N, D)) * s[None, :] / t[:, None]
    w = np.random.standard_normal((D, F)) / np.sqrt(D) / s[:, None]
    b = 0.5 * np.random.standard_normal(F)
    q = (1.0 + 0.1 * np.random.standard_normal(N)) * t
    words, scales = pack4(w)
    return {"x": bf(x), "f": bf(f), "w_words": words, "w_scales": scales, "b": bf(b), "q": bf(q)}


def core(x, f, w_words, w_scales, b, q):
    n_samples = x.shape[0]
    wq = unpack4(w_words, w_scales)
    psi = np.tanh((mxq(f64(x), 1, "e4m3") @ wq) + f64(b)[None, :])
    zd = mxq(f64(f), 1, "e4m3") @ wq
    lpsi = (1.0 - psi * psi) * zd
    a = f64(q)[:, None] * psi
    return (mxq(a, 0, "e4m3").T @ mxq(lpsi, 0, "e4m3")) / np.sqrt(n_samples)


def reference(x, f, w_words, w_scales, b, q):
    R_out = core(x, f, w_words, w_scales, b, q)
    words, scales = planes(R_out.T)
    return R_out, words, scales

@@ -1,0 +1,448 @@
+import math
+from contextlib import ExitStack
+
+import concourse.mybir as mybir
+from concourse.masks import make_identity
+
+F32 = mybir.dt.float32
+BF16 = mybir.dt.bfloat16
+I32 = mybir.dt.int32
+U32 = mybir.dt.uint32
+U8 = mybir.dt.uint8
+E4M3 = mybir.dt.float8_e4m3fn_x4
+E2M1 = mybir.dt.float4_e2m1fn_x4
+ALU = mybir.AluOpType
+ACT = mybir.ActivationFunctionType
+
+P = 128
+SAMPLES, FEATS, DICT = 2048, 512, 1024
+GROUPS = SAMPLES // 512
+BLOCKS = DICT // P
+FLOPS = 2 * 2 * SAMPLES * FEATS * DICT + 2 * SAMPLES * DICT * DICT
+NEG_SCALE = -1.0 / math.sqrt(SAMPLES)
+
+PHASES = [(0, 3), (3, 4), (4, 5), (5, 6), (6, 7), (7, 8)]
+
+
+def widths(total):
+    parts = []
+    for w in (512, 256, 128):
+        while total >= w:
+            parts.append(w)
+            total -= w
+    return parts
+
+
+def rects(lo, hi):
+    found = []
+    w = (hi - lo) * P
+    per = 512 // w
+    for i in range(0, lo, per):
+        found.append((i, min(per, lo - i), lo * P, w))
+    for half in (1, 0):
+        w = min(hi * P, 512 * (half + 1)) - 512 * half
+        if w <= 0:
+            continue
+        per = max(1, 512 // w)
+        for i in range(lo, hi, per):
+            found.append((i, min(per, hi - i), 512 * half, w))
+    return found
+
+
+def tile_generatoredmdstiffnessmatrix_x2_kernel(tc, x, f, w_words, w_scales, b, q, out_0, out_1, out_2):
+    nc = tc.nc
+    with ExitStack() as ctx:
+        keep = ctx.enter_context(tc.tile_pool(name="keep", bufs=1))
+        loads = ctx.enter_context(tc.tile_pool(name="loads", bufs=8))
+        work = ctx.enter_context(tc.tile_pool(name="work", bufs=4))
+        psum = ctx.enter_context(tc.psum_pool(name="psum", bufs=2))
+
+        ctx.enter_context(tc.manual_schedule())
+
+        warm = keep.tile([P, 1], F32, name="warm")
+        nc.vector.memset(warm[:], 0.0)
+        nc.scalar.activation(out=warm[:], in_=warm[:], func=ACT.Tanh)
+
+        ws = keep.tile([P, DICT], U8, name="ws", align_bytes=64)
+        nc.vector.memset(ws[:].bitcast(I32), 0)
+        ident = keep.tile([P, P], F32, name="ident")
+        make_identity(nc, ident[:])
+
+        raw = []
+        items = [(src, g) for g in range(GROUPS) for src in (x, f)]
+        wt = keep.tile([P, 2 * DICT], U8, name="wt", align_bytes=64)
+        bt = keep.tile([P, DICT], BF16, name="bt")
+        qt = keep.tile([P, GROUPS * 4], BF16, name="qt")
+        for n, (src, g) in enumerate(items):
+            r = loads.tile([P, 4, FEATS], BF16, name="r", align_bytes=64)
+            view = src[512 * g : 512 * (g + 1), :].rearrange("(m t) k -> m t k", t=4)
+            if n < 2:
+                for h in range(2):
+                    nc.sync.dma_start(out=r[:, 2 * h : 2 * h + 2, :], in_=view[:, 2 * h : 2 * h + 2, :])
+            else:
+                nc.sync.dma_start(out=r[:], in_=view)
+            raw.append(r)
+            if n == 0:
+                for quad in range(4):
+                    nc.sync.dma_start(
+                        out=ws[32 * quad : 32 * quad + 4, :].bitcast(I32),
+                        in_=w_scales[0, 4 * quad : 4 * quad + 4, :].bitcast(I32),
+                    )
+                nc.sync.dma_start(out=wt[:].bitcast(I32), in_=w_words[0].bitcast(I32))
+            if n == 0:
+                nc.sync.dma_start(out=bt[:], in_=b.partition_broadcast(P))
+                nc.sync.dma_start(
+                    out=qt[:].rearrange("p (g t) -> p g t", t=4), in_=q.rearrange("(g p t) -> p g t", p=P, t=4)
+                )
+
+        xc = keep.tile([P, 2 * GROUPS, 512], U32, name="xc", align_bytes=64)
+        xs = keep.tile([P, 2 * GROUPS, 512], U8, name="xs", align_bytes=64)
+        ac = keep.tile([P, GROUPS, DICT], U32, name="ac", align_bytes=64)
+        asc = keep.tile([P, GROUPS, DICT], U8, name="asc", align_bytes=64)
+        lc = keep.tile([P, GROUPS, DICT], U32, name="lc", align_bytes=64)
+        lsc = keep.tile([P, GROUPS, DICT], U8, name="lsc", align_bytes=64)
+        r32 = keep.tile([P, BLOCKS, DICT], F32, name="r32", align_bytes=64)
+        r16 = keep.tile([P, BLOCKS, DICT], BF16, name="r16", align_bytes=64)
+        pc = keep.tile([P, 2, DICT], U32, name="pc", align_bytes=64)
+        psc = keep.tile([P, 2, DICT], U8, name="psc", align_bytes=64)
+
+        banks = {}
+        grouped = {}
+
+        def turn(n):
+            pair = []
+            words = raw[n][:].rearrange("m t k -> m (t k)").bitcast(F32)
+            for h in range(2):
+                bank = psum.tile([P, 2, 2, P], F32, name="rt", bufs=4)
+                for t in range(2):
+                    for u in range(2):
+                        base = 256 * (2 * h + t)
+                        nc.tensor.transpose(bank[:, t, u, :], words[:, base + u : base + 256 : 2], ident[:])
+                pair.append(bank)
+            banks[n] = pair
+
+        def empty(n, engines):
+            xw = work.tile([P, 2048], BF16, name="xw", align_bytes=64, bufs=3)
+            for h in range(2):
+                dst = xw[:, 1024 * h : 1024 * (h + 1)].bitcast(F32).rearrange("p (t m u) -> p t m u", t=2, u=2)
+                src = banks[n][h][:].rearrange("p t u m -> p t m u")
+                if engines[h] == "s":
+                    nc.scalar.copy(out=dst, in_=src)
+                else:
+                    nc.vector.tensor_copy(out=dst, in_=src)
+            grouped[n] = xw
+
+        def quant_x(n):
+            nc.vector.quantize_mx(out=xc[:, n, :].bitcast(E4M3), scales=xs[:, n, :], in_=grouped[n][:])
+
+        chunks = []
+        for lo, hi in PHASES:
+            order = [(g, k) for g in range(GROUPS) for k in range(lo, hi)]
+            chunks.extend(order)
+        ends = [hi * GROUPS - 1 for lo, hi in PHASES]
+
+        zs, ds, us, psis, sqs, a16s, l16s = {}, {}, {}, {}, {}, {}, {}
+
+        def project(bank, n, k):
+            for t in range(4):
+                nc.tensor.matmul_mx(
+                    out=bank[:, t, :],
+                    lhsT=xc[:, n, P * t : P * (t + 1)].bitcast(E4M3),
+                    lhsT_scale=xs[:, n, P * t : P * (t + 1)],
+                    rhs=wt[:, 2 * P * k : 2 * P * (k + 1)].bitcast(E2M1),
+                    rhs_scale=ws[:, P * k : P * (k + 1)],
+                    start=True,
+                    stop=True,
+                )
+
+        def stage1z(c):
+            g, k = chunks[c]
+            z = psum.tile([P, 4, P], F32, name="z")
+            project(z, 2 * g, k)
+            zs[c] = z
+
+        def stage1d(c):
+            g, k = chunks[c]
+            d = psum.tile([P, 4, P], F32, name="d")
+            project(d, 2 * g + 1, k)
+            ds[c] = d
+
+        def bias(c):
+            g, k = chunks[c]
+            u = work.tile([P, 512], F32, name="u", bufs=3)
+            nc.vector.tensor_tensor(
+                out=u[:].rearrange("p (n t) -> p n t", t=4),
+                in0=zs[c][:].rearrange("p t n -> p n t"),
+                in1=bt[:, P * k : P * (k + 1)].unsqueeze(2).to_broadcast([P, P, 4]),
+                op=ALU.add,
+            )
+            us[c] = u
+
+        def tanh(c):
+            psi = work.tile([P, 512], F32, name="psi")
+            nc.scalar.activation(out=psi[:], in_=us[c][:], func=ACT.Tanh)
+            psis[c] = psi
+
+        def square(c):
+            sq = work.tile([P, 512], F32, name="sq", bufs=3)
+            nc.scalar.activation(out=sq[:], in_=psis[c][:], func=ACT.Square)
+            sqs[c] = sq
+
+        def weigh(c):
+            g, k = chunks[c]
+            a16 = work.tile([P, 512], BF16, name="a16", align_bytes=64)
+            nc.gpsimd.tensor_tensor(
+                out=a16[:].rearrange("p (n t) -> p n t", t=4),
+                in0=psis[c][:].rearrange("p (n t) -> p n t", t=4),
+                in1=qt[:, 4 * g : 4 * (g + 1)].unsqueeze(1).to_broadcast([P, P, 4]),
+                op=ALU.mult,
+            )
+            a16s[c] = a16
+
+        def lie(c):
+            l16 = work.tile([P, 512], BF16, name="l16", align_bytes=64)
+            nc.vector.scalar_tensor_tensor(
+                out=l16[:].rearrange("p (n t) -> p n t", t=4),
+                in0=sqs[c][:].rearrange("p (n t) -> p n t", t=4),
+                scalar=1.0,
+                in1=ds[c][:].rearrange("p t n -> p n t"),
+                op0=ALU.subtract,
+                op1=ALU.mult,
+            )
+            l16s[c] = l16
+
+        def quant(c):
+            g, k = chunks[c]
+            cols = slice(P * k, P * (k + 1))
+            nc.vector.quantize_mx(out=lc[:, g, cols].bitcast(E4M3), scales=lsc[:, g, cols], in_=l16s[c][:])
+            nc.vector.quantize_mx(out=ac[:, g, cols].bitcast(E4M3), scales=asc[:, g, cols], in_=a16s[c][:])
+
+        def stage2(rect, tag, bufs):
+            i0, rows, j0, w = rect
+            bank = psum.tile([P, 512], F32, name=tag, bufs=bufs)
+            for r in range(rows):
+                col = 0
+                for n in widths(w):
+                    for g in range(GROUPS):
+                        nc.tensor.matmul_mx(
+                            out=bank[:, r * w + col : r * w + col + n],
+                            lhsT=ac[:, g, P * (i0 + r) : P * (i0 + r + 1)].bitcast(E4M3),
+                            lhsT_scale=asc[:, g, P * (i0 + r) : P * (i0 + r + 1)],
+                            rhs=lc[:, g, j0 + col : j0 + col + n].bitcast(E4M3),
+                            rhs_scale=lsc[:, g, j0 + col : j0 + col + n],
+                            start=(g == 0),
+                            stop=(g == GROUPS - 1),
+                        )
+                    col += n
+            return bank
+
+        def late_pass(bank, half, g):
+            i = BLOCKS - 1
+            nc.tensor.matmul_mx(
+                out=bank[:],
+                lhsT=ac[:, g, P * i : P * (i + 1)].bitcast(E4M3),
+                lhsT_scale=asc[:, g, P * i : P * (i + 1)],
+                rhs=lc[:, g, 512 * half : 512 * (half + 1)].bitcast(E4M3),
+                rhs_scale=lsc[:, g, 512 * half : 512 * (half + 1)],
+                start=(g == 0),
+                stop=(g == GROUPS - 1),
+            )
+
+        def emit_r(rect, bank, engine):
+            i0, rows, j0, w = rect
+            dst = r32[:, i0 : i0 + rows, j0 : j0 + w]
+            src = bank[:, 0 : rows * w].rearrange("p (r w) -> p r w", r=rows)
+            if engine == "s":
+                nc.scalar.activation(out=dst, in_=src, func=ACT.Copy, scale=NEG_SCALE)
+            else:
+                nc.vector.tensor_scalar(out=dst, in0=src, scalar1=NEG_SCALE, scalar2=None, op0=ALU.mult)
+            for r in range(i0, i0 + rows):
+                nc.sync.dma_start(out=out_0[P * r : P * (r + 1), j0 : j0 + w], in_=r32[:, r, j0 : j0 + w])
+
+        def cast_r(rect, engine):
+            i0, rows, j0, w = rect
+            (nc.gpsimd if engine == "g" else nc.vector).tensor_scalar(
+                out=r16[:, i0 : i0 + rows, j0 : j0 + w],
+                in0=r32[:, i0 : i0 + rows, j0 : j0 + w],
+                scalar1=1.0,
+                scalar2=1.0,
+                op0=ALU.mult,
+                op1=ALU.mult,
+            )
+
+        def turn_r(pair, half, tag, bufs):
+            bank = psum.tile([P, 2, 2, P], F32, name=tag, bufs=bufs)
+            for e in range(2):
+                words = r16[:, 2 * pair + e, 512 * half : 512 * (half + 1)].bitcast(F32)
+                for u in range(2):
+                    nc.tensor.transpose(bank[:, e, u, :], words[:, u:256:2], ident[:])
+            return bank
+
+        def plane(pair, half, bank, engine):
+            pw = work.tile([P, 1024], BF16, name="pw", align_bytes=64, bufs=3)
+            dst = pw[:].bitcast(F32).rearrange("p (e m u) -> p e m u", e=2, u=2)
+            src = bank[:].rearrange("p e u m -> p e m u")
+            if engine == "s":
+                nc.scalar.copy(out=dst, in_=src)
+            else:
+                nc.vector.tensor_copy(out=dst, in_=src)
+            return pw
+
+        def quant_p(pair, half, pw):
+            cols = slice(256 * pair, 256 * (pair + 1))
+            nc.vector.quantize_mx(out=pc[:, half, cols].bitcast(E4M3), scales=psc[:, half, cols], in_=pw[:])
+            nc.sync.dma_start(
+                out=out_1[half, :, cols, :].rearrange("p m t -> p (m t)").bitcast(I32),
+                in_=pc[:, half, cols].bitcast(I32),
+            )
+
+        def store_scales(half):
+            for quad in range(4):
+                nc.sync.dma_start(
+                    out=out_2[half, 4 * quad : 4 * quad + 4, :].bitcast(I32),
+                    in_=psc[32 * quad : 32 * quad + 4, half, :].bitcast(I32),
+                )
+
+        turn(0)
+        empty(0, "sv")
+        quant_x(0)
+        stage1z(0)
+        turn(1)
+        bias(0)
+        empty(1, "sv")
+        quant_x(1)
+        stage1z(1)
+        turn(2)
+        stage1d(0)
+        tanh(0)
+        weigh(0)
+        empty(2, "ss")
+        turn(3)
+
+        total = len(chunks)
+        last_lo = PHASES[-1][0]
+        todo, made, fresh, flips, flipped, planes_q = [], [], [], [], [], []
+        cover = {}
+        left = {0: 4, 1: 4}
+        count = {"r": 0, "p": 0}
+        late = []
+        xwait = [2]
+
+        def ready(rect):
+            i0, rows, j0, w = rect
+            half = j0 // 512
+            for r in range(i0, i0 + rows):
+                cover[(r, half)] = cover.get((r, half), 0) + w
+                if cover[(r, half)] == 512 and cover.get((r ^ 1, half), 0) == 512:
+                    flips.append((r // 2, half))
+
+        def finish(pair, half, pw):
+            quant_p(pair, half, pw)
+            left[half] -= 1
+            if left[half] == 0:
+                store_scales(half)
+
+        RPAT = "s"
+        PPAT = "s"
+        XPAT = ["ss"]
+        for s in range(1, total + 2):
+            if s < total:
+                bias(s)
+            if 0 <= s - 1 < total:
+                square(s - 1)
+                lie(s - 1)
+            if s < total:
+                tanh(s)
+                weigh(s)
+            if 0 <= s - 2 < total:
+                quant(s - 2)
+            for n in xwait:
+                quant_x(n)
+            xwait = []
+            if s + 2 < len(items):
+                empty(s + 2, XPAT[s % len(XPAT)])
+                xwait.append(s + 2)
+            for args in planes_q:
+                finish(*args)
+            planes_q = []
+            for pair, half, bank in flipped:
+                planes_q.append((pair, half, plane(pair, half, bank, PPAT[count["p"] % len(PPAT)])))
+                count["p"] += 1
+            flipped = []
+            for rect, bank in made:
+                emit_r(rect, bank, RPAT[count["r"] % len(RPAT)])
+                count["r"] += 1
+                cast_r(rect, "g")
+                fresh.append((s, rect))
+            made = []
+            if s + 1 < total:
+                stage1z(s + 1)
+            if s < total:
+                stage1d(s)
+            if s + 3 < len(items):
+                turn(s + 3)
+            if s - 2 in ends[:-1]:
+                lo, hi = PHASES[ends.index(s - 2)]
+                todo.extend(rects(lo, hi))
+            g = s - 2 - (total - GROUPS)
+            for k in range(1):
+                if todo and g < 0:
+                    rect = todo.pop(0)
+                    made.append((rect, stage2(rect, "rt", 4)))
+            while fresh and fresh[0][0] < s:
+                ready(fresh.pop(0)[1])
+            if flips and not made[1:]:
+                pair, half = flips.pop(0)
+                flipped.append((pair, half, turn_r(pair, half, "rt", 4)))
+            if 0 <= g:
+                if g == 0:
+                    late = [psum.tile([P, 512], F32, name="rt", bufs=4) for half in range(2)]
+                for half in range(2):
+                    late_pass(late[half], half, g)
+                if todo:
+                    rect = todo.pop(0)
+                    made.append((rect, stage2(rect, "rt", 4)))
+
+        row = BLOCKS - 1
+        late_rects = [(row, 1, 512, 512), (row, 1, 0, 512)]
+        ra, rb = rects(last_lo, BLOCKS)[:2]
+        ba = stage2(ra, "z", 2)
+        emit_r(late_rects[1], late[0], "s")
+        emit_r(late_rects[0], late[1], "v")
+        cast_r(late_rects[1], "g")
+        cast_r(late_rects[0], "v")
+        for args in planes_q:
+            finish(*args)
+        for pair, half, bank in flipped:
+            finish(pair, half, plane(pair, half, bank, "v"))
+        for rect, bank in made:
+            emit_r(rect, bank, "s")
+            cast_r(rect, "v")
+            fresh.append((s, rect))
+        for s_, rect in fresh:
+            ready(rect)
+        while todo:
+            rect = todo.pop(0)
+            bank = stage2(rect, "rt", 4)
+            emit_r(rect, bank, "s")
+            cast_r(rect, "v")
+            ready(rect)
+        bb = stage2(rb, "z", 2)
+        emit_r(ra, ba, "s")
+        cast_r(ra, "v")
+        ready(ra)
+        ready(late_rects[1])
+        emit_r(rb, bb, "v")
+        cast_r(rb, "v")
+        ready(late_rects[0])
+        ready(rb)
+        queue = []
+        n = 0
+        for pair, half in flips:
+            bank = turn_r(pair, half, "d" if n % 2 else "rt", 2 if n % 2 else 4)
+            queue.append((pair, half, plane(pair, half, bank, "sv"[n % 2])))
+            n += 1
+            if len(queue) > 1:
+                finish(*queue.pop(0))
+        for args in queue:
+            finish(*args)

@@ -21,6 +21,7 @@ BLOCKS = DICT // P
 FLOPS = 2 * 2 * SAMPLES * FEATS * DICT + 2 * SAMPLES * DICT * DICT
 NEG_SCALE = -1.0 / math.sqrt(SAMPLES)
 
+APAT = "g"
 PHASES = [(0, 3), (3, 4), (4, 5), (5, 6), (6, 7), (7, 8)]
 
 
@@ -188,10 +189,13 @@ def tile_generatoredmdstiffnessmatrix_x2_kernel(tc, x, f, w_words, w_scales, b, 
             nc.scalar.activation(out=sq[:], in_=psis[c][:], func=ACT.Square)
             sqs[c] = sq
 
+        def on_g(c):
+            return APAT[c % len(APAT)] == "g"
+
         def weigh(c):
             g, k = chunks[c]
             a16 = work.tile([P, 512], BF16, name="a16", align_bytes=64)
-            nc.gpsimd.tensor_tensor(
+            (nc.gpsimd if on_g(c) else nc.vector).tensor_tensor(
                 out=a16[:].rearrange("p (n t) -> p n t", t=4),
                 in0=psis[c][:].rearrange("p (n t) -> p n t", t=4),
                 in1=qt[:, 4 * g : 4 * (g + 1)].unsqueeze(1).to_broadcast([P, P, 4]),
@@ -315,13 +319,14 @@ def tile_generatoredmdstiffnessmatrix_x2_kernel(tc, x, f, w_words, w_scales, b, 
         turn(2)
         stage1d(0)
         tanh(0)
-        weigh(0)
+        if on_g(0):
+            weigh(0)
         empty(2, "ss")
         turn(3)
 
         total = len(chunks)
         last_lo = PHASES[-1][0]
-        todo, made, fresh, flips, flipped, planes_q = [], [], [], [], [], []
+        todo, made, fresh, flips, flipped, planes_q, casts = [], [], [], [], [], [], []
         cover = {}
         left = {0: 4, 1: 4}
         count = {"r": 0, "p": 0}
@@ -350,21 +355,29 @@ def tile_generatoredmdstiffnessmatrix_x2_kernel(tc, x, f, w_words, w_scales, b, 
                 bias(s)
             if 0 <= s - 1 < total:
                 square(s - 1)
-                lie(s - 1)
             if s < total:
                 tanh(s)
-                weigh(s)
+                if on_g(s):
+                    weigh(s)
+            if s - 1 < total and not on_g(s - 1):
+                weigh(s - 1)
             if 0 <= s - 2 < total:
                 quant(s - 2)
+            for rect in casts:
+                cast_r(rect, "v")
+                ready(rect)
+            casts = []
             for n in xwait:
                 quant_x(n)
             xwait = []
-            if s + 2 < len(items):
-                empty(s + 2, XPAT[s % len(XPAT)])
-                xwait.append(s + 2)
             for args in planes_q:
                 finish(*args)
             planes_q = []
+            if 0 <= s - 1 < total:
+                lie(s - 1)
+            if s + 2 < len(items):
+                empty(s + 2, XPAT[s % len(XPAT)])
+                xwait.append(s + 2)
             for pair, half, bank in flipped:
                 planes_q.append((pair, half, plane(pair, half, bank, PPAT[count["p"] % len(PPAT)])))
                 count["p"] += 1
@@ -372,8 +385,7 @@ def tile_generatoredmdstiffnessmatrix_x2_kernel(tc, x, f, w_words, w_scales, b, 
             for rect, bank in made:
                 emit_r(rect, bank, RPAT[count["r"] % len(RPAT)])
                 count["r"] += 1
-                cast_r(rect, "g")
-                fresh.append((s, rect))
+                casts.append(rect)
             made = []
             if s + 1 < total:
                 stage1z(s + 1)
@@ -389,8 +401,6 @@ def tile_generatoredmdstiffnessmatrix_x2_kernel(tc, x, f, w_words, w_scales, b, 
                 if todo and g < 0:
                     rect = todo.pop(0)
                     made.append((rect, stage2(rect, "rt", 4)))
-            while fresh and fresh[0][0] < s:
-                ready(fresh.pop(0)[1])
             if flips and not made[1:]:
                 pair, half = flips.pop(0)
                 flipped.append((pair, half, turn_r(pair, half, "rt", 4)))
@@ -406,9 +416,16 @@ def tile_generatoredmdstiffnessmatrix_x2_kernel(tc, x, f, w_words, w_scales, b, 
         row = BLOCKS - 1
         late_rects = [(row, 1, 512, 512), (row, 1, 0, 512)]
         ra, rb = rects(last_lo, BLOCKS)[:2]
+        for g in range(total + 2 - 2 - (total - GROUPS), GROUPS):
+            for half in range(2):
+                late_pass(late[half], half, g)
         ba = stage2(ra, "z", 2)
+        bb = stage2(rb, "z", 2)
         emit_r(late_rects[1], late[0], "s")
         emit_r(late_rects[0], late[1], "v")
+        for rect in casts:
+            cast_r(rect, "v")
+            ready(rect)
         cast_r(late_rects[1], "g")
         cast_r(late_rects[0], "v")
         for args in planes_q:
@@ -418,8 +435,6 @@ def tile_generatoredmdstiffnessmatrix_x2_kernel(tc, x, f, w_words, w_scales, b, 
         for rect, bank in made:
             emit_r(rect, bank, "s")
             cast_r(rect, "v")
-            fresh.append((s, rect))
-        for s_, rect in fresh:
             ready(rect)
         while todo:
             rect = todo.pop(0)
@@ -427,7 +442,6 @@ def tile_generatoredmdstiffnessmatrix_x2_kernel(tc, x, f, w_words, w_scales, b, 
             emit_r(rect, bank, "s")
             cast_r(rect, "v")
             ready(rect)
-        bb = stage2(rb, "z", 2)
         emit_r(ra, ba, "s")
         cast_r(ra, "v")
         ready(ra)

@@ -21,6 +21,8 @@ BLOCKS = DICT // P
 FLOPS = 2 * 2 * SAMPLES * FEATS * DICT + 2 * SAMPLES * DICT * DICT
 NEG_SCALE = -1.0 / math.sqrt(SAMPLES)
 
+SPIN = [0] + [1] * 11
+SPIN0 = 7
 APAT = "g"
 PHASES = [(0, 3), (3, 4), (4, 5), (5, 6), (6, 7), (7, 8)]
 
@@ -66,8 +68,17 @@ def tile_generatoredmdstiffnessmatrix_x2_kernel(tc, x, f, w_words, w_scales, b, 
 
         ws = keep.tile([P, DICT], U8, name="ws", align_bytes=64)
         nc.vector.memset(ws[:].bitcast(I32), 0)
+        brow = keep.tile([P, P], BF16, name="brow")
+        nc.vector.memset(brow[:], 0.0)
+        xc = keep.tile([P, 2 * GROUPS, 512], U32, name="xc", align_bytes=64)
+        xs = keep.tile([P, 2 * GROUPS, 512], U8, name="xs", align_bytes=64)
+        nc.vector.memset(xc[:, 2 * GROUPS - 1, :].bitcast(I32), 0)
+        nc.vector.memset(xs[:, 2 * GROUPS - 1, :].bitcast(I32), 0)
         ident = keep.tile([P, P], F32, name="ident")
         make_identity(nc, ident[:])
+        identb = keep.tile([P, P], BF16, name="identb")
+        nc.vector.tensor_copy(out=identb[:], in_=ident[:])
+        nc.sync.dma_start(out=brow[0:BLOCKS, :], in_=b.rearrange("(k n) -> k n", n=P))
 
         raw = []
         items = [(src, g) for g in range(GROUPS) for src in (x, f)]
@@ -90,14 +101,11 @@ def tile_generatoredmdstiffnessmatrix_x2_kernel(tc, x, f, w_words, w_scales, b, 
                         in_=w_scales[0, 4 * quad : 4 * quad + 4, :].bitcast(I32),
                     )
                 nc.sync.dma_start(out=wt[:].bitcast(I32), in_=w_words[0].bitcast(I32))
-            if n == 0:
-                nc.sync.dma_start(out=bt[:], in_=b.partition_broadcast(P))
+            if n == 1:
                 nc.sync.dma_start(
                     out=qt[:].rearrange("p (g t) -> p g t", t=4), in_=q.rearrange("(g p t) -> p g t", p=P, t=4)
                 )
 
-        xc = keep.tile([P, 2 * GROUPS, 512], U32, name="xc", align_bytes=64)
-        xs = keep.tile([P, 2 * GROUPS, 512], U8, name="xs", align_bytes=64)
         ac = keep.tile([P, GROUPS, DICT], U32, name="ac", align_bytes=64)
         asc = keep.tile([P, GROUPS, DICT], U8, name="asc", align_bytes=64)
         lc = keep.tile([P, GROUPS, DICT], U32, name="lc", align_bytes=64)
@@ -110,31 +118,37 @@ def tile_generatoredmdstiffnessmatrix_x2_kernel(tc, x, f, w_words, w_scales, b, 
         banks = {}
         grouped = {}
 
-        def turn(n):
-            pair = []
+        def turn(n, h):
             words = raw[n][:].rearrange("m t k -> m (t k)").bitcast(F32)
-            for h in range(2):
-                bank = psum.tile([P, 2, 2, P], F32, name="rt", bufs=4)
-                for t in range(2):
-                    for u in range(2):
-                        base = 256 * (2 * h + t)
-                        nc.tensor.transpose(bank[:, t, u, :], words[:, base + u : base + 256 : 2], ident[:])
-                pair.append(bank)
-            banks[n] = pair
+            bank = psum.tile([P, 2, 2, P], F32, name="rt", bufs=4)
+            for t in range(2):
+                for u in range(2):
+                    base = 256 * (2 * h + t)
+                    nc.tensor.transpose(bank[:, t, u, :], words[:, base + u : base + 256 : 2], ident[:])
+            banks[n, h] = bank
 
-        def empty(n, engines):
-            xw = work.tile([P, 2048], BF16, name="xw", align_bytes=64, bufs=3)
-            for h in range(2):
-                dst = xw[:, 1024 * h : 1024 * (h + 1)].bitcast(F32).rearrange("p (t m u) -> p t m u", t=2, u=2)
-                src = banks[n][h][:].rearrange("p t u m -> p t m u")
-                if engines[h] == "s":
-                    nc.scalar.copy(out=dst, in_=src)
-                else:
-                    nc.vector.tensor_copy(out=dst, in_=src)
-            grouped[n] = xw
+        def empty(n, h, engine):
+            if h == 0:
+                xw = work.tile([P, 2048], BF16, name="xw", align_bytes=64, bufs=3)
+                grouped[n] = xw
+            dst = grouped[n][:, 1024 * h : 1024 * (h + 1)].bitcast(F32).rearrange("p (t m u) -> p t m u", t=2, u=2)
+            src = banks[n, h][:].rearrange("p t u m -> p t m u")
+            if engine == "s":
+                nc.scalar.copy(out=dst, in_=src)
+            else:
+                nc.vector.tensor_copy(out=dst, in_=src)
 
-        def quant_x(n):
-            nc.vector.quantize_mx(out=xc[:, n, :].bitcast(E4M3), scales=xs[:, n, :], in_=grouped[n][:])
+        def quant_x(n, parts=1):
+            w = 512 // parts
+            for h in range(parts):
+                quant_x_part(n, slice(w * h, w * (h + 1)))
+
+        def quant_x_part(n, cols):
+            nc.vector.quantize_mx(
+                out=xc[:, n, cols].bitcast(E4M3),
+                scales=xs[:, n, cols],
+                in_=grouped[n][:, 4 * cols.start : 4 * cols.stop],
+            )
 
         chunks = []
         for lo, hi in PHASES:
@@ -143,6 +157,18 @@ def tile_generatoredmdstiffnessmatrix_x2_kernel(tc, x, f, w_words, w_scales, b, 
         ends = [hi * GROUPS - 1 for lo, hi in PHASES]
 
         zs, ds, us, psis, sqs, a16s, l16s = {}, {}, {}, {}, {}, {}, {}
+
+        def spin(out):
+            n = 2 * GROUPS - 1
+            nc.tensor.matmul_mx(
+                out=out,
+                lhsT=xc[:, n, 0:P].bitcast(E4M3),
+                lhsT_scale=xs[:, n, 0:P],
+                rhs=xc[:, n, :].bitcast(E4M3),
+                rhs_scale=xs[:, n, :],
+                start=True,
+                stop=True,
+            )
 
         def project(bank, n, k):
             for t in range(4):
@@ -159,6 +185,8 @@ def tile_generatoredmdstiffnessmatrix_x2_kernel(tc, x, f, w_words, w_scales, b, 
         def stage1z(c):
             g, k = chunks[c]
             z = psum.tile([P, 4, P], F32, name="z")
+            for r in range(SPIN[c] if c < len(SPIN) else 0):
+                spin(z[:].rearrange("p t n -> p (t n)"))
             project(z, 2 * g, k)
             zs[c] = z
 
@@ -190,7 +218,7 @@ def tile_generatoredmdstiffnessmatrix_x2_kernel(tc, x, f, w_words, w_scales, b, 
             sqs[c] = sq
 
         def on_g(c):
-            return APAT[c % len(APAT)] == "g"
+            return c > 0 and APAT[c % len(APAT)] == "g"
 
         def weigh(c):
             g, k = chunks[c]
@@ -307,22 +335,44 @@ def tile_generatoredmdstiffnessmatrix_x2_kernel(tc, x, f, w_words, w_scales, b, 
                     in_=psc[32 * quad : 32 * quad + 4, half, :].bitcast(I32),
                 )
 
-        turn(0)
-        empty(0, "sv")
-        quant_x(0)
+        plan = {1: [(2, 0), (2, 1)], 2: [(3, 0), (3, 1)], 3: [(4, 0)], 4: [(4, 1), (5, 0)], 5: [(5, 1)], 6: [(6, 0)], 7: [(6, 1), (7, 0)], 8: [(7, 1)]}
+        half0, half1 = slice(0, 256), slice(256, 512)
+        idle = psum.tile([P, 512], F32, name="d")
+        for r in range(SPIN0):
+            spin(idle[:])
+        bcol = keep.tile([P, BLOCKS], BF16, name="bcol")
+        bank = psum.tile([P, P], BF16, name="rt", bufs=4)
+        nc.tensor.transpose(bank[:], brow[:], identb[:])
+        nc.vector.tensor_copy(out=bcol[:], in_=bank[:, 0:BLOCKS])
+        turn(0, 0)
+        turn(0, 1)
+        spread = psum.tile([P, DICT], BF16, name="rt", bufs=4)
+        for k in range(BLOCKS):
+            nc.tensor.transpose(spread[:, P * k : P * (k + 1)], bcol[:, k : k + 1].to_broadcast([P, P]), identb[:])
+        empty(0, 0, "s")
+        empty(0, 1, "v")
+        quant_x_part(0, half0)
+        quant_x_part(0, half1)
+        nc.scalar.copy(out=bt[:, 0:256], in_=spread[:, 0:256])
+        turn(1, 0)
+        for r in range(1):
+            spin(idle[:])
         stage1z(0)
-        turn(1)
+        turn(1, 1)
+        empty(1, 0, "s")
         bias(0)
-        empty(1, "sv")
-        quant_x(1)
         stage1z(1)
-        turn(2)
-        stage1d(0)
+        empty(1, 1, "v")
         tanh(0)
-        if on_g(0):
-            weigh(0)
-        empty(2, "ss")
-        turn(3)
+        quant_x_part(1, half0)
+        quant_x_part(1, half1)
+        for r in range(1):
+            spin(idle[:])
+        nc.scalar.copy(out=bt[:, 256:DICT], in_=spread[:, 256:DICT])
+        square(0)
+        stage1d(0)
+        for n, h in plan[1]:
+            turn(n, h)
 
         total = len(chunks)
         last_lo = PHASES[-1][0]
@@ -331,7 +381,7 @@ def tile_generatoredmdstiffnessmatrix_x2_kernel(tc, x, f, w_words, w_scales, b, 
         left = {0: 4, 1: 4}
         count = {"r": 0, "p": 0}
         late = []
-        xwait = [2]
+        xwait = []
 
         def ready(rect):
             i0, rows, j0, w = rect
@@ -349,11 +399,11 @@ def tile_generatoredmdstiffnessmatrix_x2_kernel(tc, x, f, w_words, w_scales, b, 
 
         RPAT = "s"
         PPAT = "s"
-        XPAT = ["ss"]
+        XPAT = ["s"]
         for s in range(1, total + 2):
             if s < total:
                 bias(s)
-            if 0 <= s - 1 < total:
+            if 1 <= s - 1 < total:
                 square(s - 1)
             if s < total:
                 tanh(s)
@@ -375,9 +425,10 @@ def tile_generatoredmdstiffnessmatrix_x2_kernel(tc, x, f, w_words, w_scales, b, 
             planes_q = []
             if 0 <= s - 1 < total:
                 lie(s - 1)
-            if s + 2 < len(items):
-                empty(s + 2, XPAT[s % len(XPAT)])
-                xwait.append(s + 2)
+            for n, h in plan.get(s, []):
+                empty(n, h, XPAT[(2 * n + h) % len(XPAT)])
+                if h == 1:
+                    xwait.append(n)
             for pair, half, bank in flipped:
                 planes_q.append((pair, half, plane(pair, half, bank, PPAT[count["p"] % len(PPAT)])))
                 count["p"] += 1
@@ -391,8 +442,8 @@ def tile_generatoredmdstiffnessmatrix_x2_kernel(tc, x, f, w_words, w_scales, b, 
                 stage1z(s + 1)
             if s < total:
                 stage1d(s)
-            if s + 3 < len(items):
-                turn(s + 3)
+            for n, h in plan.get(s + 1, []):
+                turn(n, h)
             if s - 2 in ends[:-1]:
                 lo, hi = PHASES[ends.index(s - 2)]
                 todo.extend(rects(lo, hi))

@@ -20,11 +20,7 @@ GROUPS = SAMPLES // 512
 BLOCKS = DICT // P
 FLOPS = 2 * 2 * SAMPLES * FEATS * DICT + 2 * SAMPLES * DICT * DICT
 NEG_SCALE = -1.0 / math.sqrt(SAMPLES)
-
-SPIN = [0] + [1] * 11
-SPIN0 = 7
-APAT = "g"
-PHASES = [(0, 3), (3, 4), (4, 5), (5, 6), (6, 7), (7, 8)]
+SPANS = [(0, 4), (4, 5), (5, 6), (6, 7), (7, 8)]
 
 
 def widths(total):
@@ -59,32 +55,26 @@ def tile_generatoredmdstiffnessmatrix_x2_kernel(tc, x, f, w_words, w_scales, b, 
         loads = ctx.enter_context(tc.tile_pool(name="loads", bufs=8))
         work = ctx.enter_context(tc.tile_pool(name="work", bufs=4))
         psum = ctx.enter_context(tc.psum_pool(name="psum", bufs=2))
-
         ctx.enter_context(tc.manual_schedule())
 
         warm = keep.tile([P, 1], F32, name="warm")
         nc.vector.memset(warm[:], 0.0)
         nc.scalar.activation(out=warm[:], in_=warm[:], func=ACT.Tanh)
-
-        ws = keep.tile([P, DICT], U8, name="ws", align_bytes=64)
-        nc.vector.memset(ws[:].bitcast(I32), 0)
-        brow = keep.tile([P, P], BF16, name="brow")
-        nc.vector.memset(brow[:], 0.0)
         xc = keep.tile([P, 2 * GROUPS, 512], U32, name="xc", align_bytes=64)
         xs = keep.tile([P, 2 * GROUPS, 512], U8, name="xs", align_bytes=64)
-        nc.vector.memset(xc[:, 2 * GROUPS - 1, :].bitcast(I32), 0)
-        nc.vector.memset(xs[:, 2 * GROUPS - 1, :].bitcast(I32), 0)
+        brow = keep.tile([P, P], BF16, name="brow")
+        nc.vector.memset(brow[:], 0.0)
+        ws = keep.tile([P, DICT], U8, name="ws", align_bytes=64)
+        nc.vector.memset(ws[:].bitcast(I32), 0)
         ident = keep.tile([P, P], F32, name="ident")
         make_identity(nc, ident[:])
         identb = keep.tile([P, P], BF16, name="identb")
         nc.vector.tensor_copy(out=identb[:], in_=ident[:])
-        nc.sync.dma_start(out=brow[0:BLOCKS, :], in_=b.rearrange("(k n) -> k n", n=P))
 
+        wt = keep.tile([P, 2 * DICT], U8, name="wt", align_bytes=64)
+        qt = keep.tile([P, GROUPS * 4], BF16, name="qt")
         raw = []
         items = [(src, g) for g in range(GROUPS) for src in (x, f)]
-        wt = keep.tile([P, 2 * DICT], U8, name="wt", align_bytes=64)
-        bt = keep.tile([P, DICT], BF16, name="bt")
-        qt = keep.tile([P, GROUPS * 4], BF16, name="qt")
         for n, (src, g) in enumerate(items):
             r = loads.tile([P, 4, FEATS], BF16, name="r", align_bytes=64)
             view = src[512 * g : 512 * (g + 1), :].rearrange("(m t) k -> m t k", t=4)
@@ -95,6 +85,7 @@ def tile_generatoredmdstiffnessmatrix_x2_kernel(tc, x, f, w_words, w_scales, b, 
                 nc.sync.dma_start(out=r[:], in_=view)
             raw.append(r)
             if n == 0:
+                nc.sync.dma_start(out=brow[0:BLOCKS, :], in_=b.rearrange("(k n) -> k n", n=P))
                 for quad in range(4):
                     nc.sync.dma_start(
                         out=ws[32 * quad : 32 * quad + 4, :].bitcast(I32),
@@ -115,8 +106,13 @@ def tile_generatoredmdstiffnessmatrix_x2_kernel(tc, x, f, w_words, w_scales, b, 
         pc = keep.tile([P, 2, DICT], U32, name="pc", align_bytes=64)
         psc = keep.tile([P, 2, DICT], U8, name="psc", align_bytes=64)
 
-        banks = {}
-        grouped = {}
+        banks, grouped = {}, {}
+
+        def pull(engine, dst, src):
+            if engine == "s":
+                nc.scalar.copy(out=dst, in_=src)
+            else:
+                nc.vector.tensor_copy(out=dst, in_=src)
 
         def turn(n, h):
             words = raw[n][:].rearrange("m t k -> m (t k)").bitcast(F32)
@@ -132,48 +128,43 @@ def tile_generatoredmdstiffnessmatrix_x2_kernel(tc, x, f, w_words, w_scales, b, 
                 xw = work.tile([P, 2048], BF16, name="xw", align_bytes=64, bufs=3)
                 grouped[n] = xw
             dst = grouped[n][:, 1024 * h : 1024 * (h + 1)].bitcast(F32).rearrange("p (t m u) -> p t m u", t=2, u=2)
-            src = banks[n, h][:].rearrange("p t u m -> p t m u")
-            if engine == "s":
-                nc.scalar.copy(out=dst, in_=src)
-            else:
-                nc.vector.tensor_copy(out=dst, in_=src)
+            pull(engine, dst, banks[n, h][:].rearrange("p t u m -> p t m u"))
 
-        def quant_x(n, parts=1):
-            w = 512 // parts
-            for h in range(parts):
-                quant_x_part(n, slice(w * h, w * (h + 1)))
-
-        def quant_x_part(n, cols):
+        def quant_x(n, cols):
             nc.vector.quantize_mx(
                 out=xc[:, n, cols].bitcast(E4M3),
                 scales=xs[:, n, cols],
                 in_=grouped[n][:, 4 * cols.start : 4 * cols.stop],
             )
 
-        chunks = []
-        for lo, hi in PHASES:
-            order = [(g, k) for g in range(GROUPS) for k in range(lo, hi)]
-            chunks.extend(order)
-        ends = [hi * GROUPS - 1 for lo, hi in PHASES]
+        chunks = [(g, k) for lo, hi in SPANS for g in range(GROUPS) for k in range(lo, hi)]
+        total = len(chunks)
+        pairs = total // 2
+        ends = [hi * GROUPS - 1 for lo, hi in SPANS]
+        zs, ds, psis, lifted, sqs, a16s, l16s = {}, {}, {}, {}, {}, {}, {}
 
-        zs, ds, us, psis, sqs, a16s, l16s = {}, {}, {}, {}, {}, {}, {}
+        def project_t(c, times):
+            g, k = chunks[c]
+            zt = psum.tile([P, 512], F32, name="z")
+            for r in range(times):
+                nc.tensor.matmul_mx(
+                    out=zt[:],
+                    lhsT=wt[:, 2 * P * k : 2 * P * (k + 1)].bitcast(E2M1),
+                    lhsT_scale=ws[:, P * k : P * (k + 1)],
+                    rhs=xc[:, 2 * g, :].bitcast(E4M3),
+                    rhs_scale=xs[:, 2 * g, :],
+                    start=True,
+                    stop=True,
+                )
+            zs[c] = zt
 
-        def spin(out):
-            n = 2 * GROUPS - 1
-            nc.tensor.matmul_mx(
-                out=out,
-                lhsT=xc[:, n, 0:P].bitcast(E4M3),
-                lhsT_scale=xs[:, n, 0:P],
-                rhs=xc[:, n, :].bitcast(E4M3),
-                rhs_scale=xs[:, n, :],
-                start=True,
-                stop=True,
-            )
-
-        def project(bank, n, k):
+        def project(c):
+            g, k = chunks[c]
+            n = 2 * g + 1
+            d = psum.tile([P, 4, P], F32, name="d")
             for t in range(4):
                 nc.tensor.matmul_mx(
-                    out=bank[:, t, :],
+                    out=d[:, t, :],
                     lhsT=xc[:, n, P * t : P * (t + 1)].bitcast(E4M3),
                     lhsT_scale=xs[:, n, P * t : P * (t + 1)],
                     rhs=wt[:, 2 * P * k : 2 * P * (k + 1)].bitcast(E2M1),
@@ -181,51 +172,34 @@ def tile_generatoredmdstiffnessmatrix_x2_kernel(tc, x, f, w_words, w_scales, b, 
                     start=True,
                     stop=True,
                 )
-
-        def stage1z(c):
-            g, k = chunks[c]
-            z = psum.tile([P, 4, P], F32, name="z")
-            for r in range(SPIN[c] if c < len(SPIN) else 0):
-                spin(z[:].rearrange("p t n -> p (t n)"))
-            project(z, 2 * g, k)
-            zs[c] = z
-
-        def stage1d(c):
-            g, k = chunks[c]
-            d = psum.tile([P, 4, P], F32, name="d")
-            project(d, 2 * g + 1, k)
             ds[c] = d
 
-        def bias(c):
-            g, k = chunks[c]
-            u = work.tile([P, 512], F32, name="u", bufs=3)
-            nc.vector.tensor_tensor(
-                out=u[:].rearrange("p (n t) -> p n t", t=4),
-                in0=zs[c][:].rearrange("p t n -> p n t"),
-                in1=bt[:, P * k : P * (k + 1)].unsqueeze(2).to_broadcast([P, P, 4]),
-                op=ALU.add,
-            )
-            us[c] = u
-
         def tanh(c):
-            psi = work.tile([P, 512], F32, name="psi")
-            nc.scalar.activation(out=psi[:], in_=us[c][:], func=ACT.Tanh)
+            g, k = chunks[c]
+            psi = work.tile([P, 512], F32, name="psi", bufs=4)
+            nc.scalar.activation(out=psi[:], in_=zs[c][:], func=ACT.Tanh, bias=bcol[:, k : k + 1])
             psis[c] = psi
 
-        def square(c):
-            sq = work.tile([P, 512], F32, name="sq", bufs=3)
-            nc.scalar.activation(out=sq[:], in_=psis[c][:], func=ACT.Square)
-            sqs[c] = sq
+        def lift(c):
+            bank = psum.tile([P, 4, P], F32, name="rt", bufs=4)
+            for t in range(4):
+                nc.tensor.transpose(bank[:, t, :], psis[c][:, P * t : P * (t + 1)], ident[:])
+            lifted[c] = bank
 
-        def on_g(c):
-            return c > 0 and APAT[c % len(APAT)] == "g"
+        def inner(tile):
+            return tile[:].rearrange("p (n t) -> p n t", t=4)
+
+        def square(c):
+            sq = work.tile([P, 512], F32, name="sq", bufs=4)
+            nc.scalar.activation(out=inner(sq), in_=lifted[c][:].rearrange("p t n -> p n t"), func=ACT.Square)
+            sqs[c] = sq
 
         def weigh(c):
             g, k = chunks[c]
             a16 = work.tile([P, 512], BF16, name="a16", align_bytes=64)
-            (nc.gpsimd if on_g(c) else nc.vector).tensor_tensor(
-                out=a16[:].rearrange("p (n t) -> p n t", t=4),
-                in0=psis[c][:].rearrange("p (n t) -> p n t", t=4),
+            nc.vector.tensor_tensor(
+                out=inner(a16),
+                in0=lifted[c][:].rearrange("p t n -> p n t"),
                 in1=qt[:, 4 * g : 4 * (g + 1)].unsqueeze(1).to_broadcast([P, P, 4]),
                 op=ALU.mult,
             )
@@ -234,8 +208,8 @@ def tile_generatoredmdstiffnessmatrix_x2_kernel(tc, x, f, w_words, w_scales, b, 
         def lie(c):
             l16 = work.tile([P, 512], BF16, name="l16", align_bytes=64)
             nc.vector.scalar_tensor_tensor(
-                out=l16[:].rearrange("p (n t) -> p n t", t=4),
-                in0=sqs[c][:].rearrange("p (n t) -> p n t", t=4),
+                out=inner(l16),
+                in0=inner(sqs[c]),
                 scalar=1.0,
                 in1=ds[c][:].rearrange("p t n -> p n t"),
                 op0=ALU.subtract,
@@ -243,11 +217,21 @@ def tile_generatoredmdstiffnessmatrix_x2_kernel(tc, x, f, w_words, w_scales, b, 
             )
             l16s[c] = l16
 
-        def quant(c):
+        def quant(codes, scales, src, c):
             g, k = chunks[c]
             cols = slice(P * k, P * (k + 1))
-            nc.vector.quantize_mx(out=lc[:, g, cols].bitcast(E4M3), scales=lsc[:, g, cols], in_=l16s[c][:])
-            nc.vector.quantize_mx(out=ac[:, g, cols].bitcast(E4M3), scales=asc[:, g, cols], in_=a16s[c][:])
+            nc.vector.quantize_mx(out=codes[:, g, cols].bitcast(E4M3), scales=scales[:, g, cols], in_=src[c][:])
+
+        def gram(bank, col, i, j0, n, g):
+            nc.tensor.matmul_mx(
+                out=bank[:, col : col + n],
+                lhsT=ac[:, g, P * i : P * (i + 1)].bitcast(E4M3),
+                lhsT_scale=asc[:, g, P * i : P * (i + 1)],
+                rhs=lc[:, g, j0 : j0 + n].bitcast(E4M3),
+                rhs_scale=lsc[:, g, j0 : j0 + n],
+                start=(g == 0),
+                stop=(g == GROUPS - 1),
+            )
 
         def stage2(rect, tag, bufs):
             i0, rows, j0, w = rect
@@ -256,29 +240,9 @@ def tile_generatoredmdstiffnessmatrix_x2_kernel(tc, x, f, w_words, w_scales, b, 
                 col = 0
                 for n in widths(w):
                     for g in range(GROUPS):
-                        nc.tensor.matmul_mx(
-                            out=bank[:, r * w + col : r * w + col + n],
-                            lhsT=ac[:, g, P * (i0 + r) : P * (i0 + r + 1)].bitcast(E4M3),
-                            lhsT_scale=asc[:, g, P * (i0 + r) : P * (i0 + r + 1)],
-                            rhs=lc[:, g, j0 + col : j0 + col + n].bitcast(E4M3),
-                            rhs_scale=lsc[:, g, j0 + col : j0 + col + n],
-                            start=(g == 0),
-                            stop=(g == GROUPS - 1),
-                        )
+                        gram(bank, r * w + col, i0 + r, j0 + col, n, g)
                     col += n
             return bank
-
-        def late_pass(bank, half, g):
-            i = BLOCKS - 1
-            nc.tensor.matmul_mx(
-                out=bank[:],
-                lhsT=ac[:, g, P * i : P * (i + 1)].bitcast(E4M3),
-                lhsT_scale=asc[:, g, P * i : P * (i + 1)],
-                rhs=lc[:, g, 512 * half : 512 * (half + 1)].bitcast(E4M3),
-                rhs_scale=lsc[:, g, 512 * half : 512 * (half + 1)],
-                start=(g == 0),
-                stop=(g == GROUPS - 1),
-            )
 
         def emit_r(rect, bank, engine):
             i0, rows, j0, w = rect
@@ -293,14 +257,12 @@ def tile_generatoredmdstiffnessmatrix_x2_kernel(tc, x, f, w_words, w_scales, b, 
 
         def cast_r(rect, engine):
             i0, rows, j0, w = rect
-            (nc.gpsimd if engine == "g" else nc.vector).tensor_scalar(
-                out=r16[:, i0 : i0 + rows, j0 : j0 + w],
-                in0=r32[:, i0 : i0 + rows, j0 : j0 + w],
-                scalar1=1.0,
-                scalar2=1.0,
-                op0=ALU.mult,
-                op1=ALU.mult,
-            )
+            src = r32[:, i0 : i0 + rows, j0 : j0 + w]
+            dst = r16[:, i0 : i0 + rows, j0 : j0 + w]
+            if engine == "g":
+                nc.gpsimd.tensor_scalar(out=dst, in0=src, scalar1=1.0, scalar2=1.0, op0=ALU.mult, op1=ALU.mult)
+            else:
+                nc.vector.tensor_copy(out=dst, in_=src)
 
         def turn_r(pair, half, tag, bufs):
             bank = psum.tile([P, 2, 2, P], F32, name=tag, bufs=bufs)
@@ -310,179 +272,171 @@ def tile_generatoredmdstiffnessmatrix_x2_kernel(tc, x, f, w_words, w_scales, b, 
                     nc.tensor.transpose(bank[:, e, u, :], words[:, u:256:2], ident[:])
             return bank
 
-        def plane(pair, half, bank, engine):
-            pw = work.tile([P, 1024], BF16, name="pw", align_bytes=64, bufs=3)
+        def plane(bank, engine):
+            pw = work.tile([P, 1024], BF16, name="pw", align_bytes=64)
             dst = pw[:].bitcast(F32).rearrange("p (e m u) -> p e m u", e=2, u=2)
-            src = bank[:].rearrange("p e u m -> p e m u")
-            if engine == "s":
-                nc.scalar.copy(out=dst, in_=src)
-            else:
-                nc.vector.tensor_copy(out=dst, in_=src)
+            pull(engine, dst, bank[:].rearrange("p e u m -> p e m u"))
             return pw
 
-        def quant_p(pair, half, pw):
+        left = {0: 4, 1: 4}
+
+        def finish(pair, half, pw):
             cols = slice(256 * pair, 256 * (pair + 1))
             nc.vector.quantize_mx(out=pc[:, half, cols].bitcast(E4M3), scales=psc[:, half, cols], in_=pw[:])
             nc.sync.dma_start(
                 out=out_1[half, :, cols, :].rearrange("p m t -> p (m t)").bitcast(I32),
                 in_=pc[:, half, cols].bitcast(I32),
             )
+            left[half] -= 1
+            if left[half] == 0:
+                for quad in range(4):
+                    nc.sync.dma_start(
+                        out=out_2[half, 4 * quad : 4 * quad + 4, :].bitcast(I32),
+                        in_=psc[32 * quad : 32 * quad + 4, half, :].bitcast(I32),
+                    )
 
-        def store_scales(half):
-            for quad in range(4):
-                nc.sync.dma_start(
-                    out=out_2[half, 4 * quad : 4 * quad + 4, :].bitcast(I32),
-                    in_=psc[32 * quad : 32 * quad + 4, half, :].bitcast(I32),
-                )
-
-        plan = {1: [(2, 0), (2, 1)], 2: [(3, 0), (3, 1)], 3: [(4, 0)], 4: [(4, 1), (5, 0)], 5: [(5, 1)], 6: [(6, 0)], 7: [(6, 1), (7, 0)], 8: [(7, 1)]}
-        half0, half1 = slice(0, 256), slice(256, 512)
-        idle = psum.tile([P, 512], F32, name="d")
-        for r in range(SPIN0):
-            spin(idle[:])
-        bcol = keep.tile([P, BLOCKS], BF16, name="bcol")
-        bank = psum.tile([P, P], BF16, name="rt", bufs=4)
-        nc.tensor.transpose(bank[:], brow[:], identb[:])
-        nc.vector.tensor_copy(out=bcol[:], in_=bank[:, 0:BLOCKS])
-        turn(0, 0)
-        turn(0, 1)
-        spread = psum.tile([P, DICT], BF16, name="rt", bufs=4)
-        for k in range(BLOCKS):
-            nc.tensor.transpose(spread[:, P * k : P * (k + 1)], bcol[:, k : k + 1].to_broadcast([P, P]), identb[:])
-        empty(0, 0, "s")
-        empty(0, 1, "v")
-        quant_x_part(0, half0)
-        quant_x_part(0, half1)
-        nc.scalar.copy(out=bt[:, 0:256], in_=spread[:, 0:256])
-        turn(1, 0)
-        for r in range(1):
-            spin(idle[:])
-        stage1z(0)
-        turn(1, 1)
-        empty(1, 0, "s")
-        bias(0)
-        stage1z(1)
-        empty(1, 1, "v")
-        tanh(0)
-        quant_x_part(1, half0)
-        quant_x_part(1, half1)
-        for r in range(1):
-            spin(idle[:])
-        nc.scalar.copy(out=bt[:, 256:DICT], in_=spread[:, 256:DICT])
-        square(0)
-        stage1d(0)
-        for n, h in plan[1]:
-            turn(n, h)
-
-        total = len(chunks)
-        last_lo = PHASES[-1][0]
-        todo, made, fresh, flips, flipped, planes_q, casts = [], [], [], [], [], [], []
-        cover = {}
-        left = {0: 4, 1: 4}
-        count = {"r": 0, "p": 0}
-        late = []
-        xwait = []
+        flips, cover = [], {}
 
         def ready(rect):
             i0, rows, j0, w = rect
             half = j0 // 512
             for r in range(i0, i0 + rows):
-                cover[(r, half)] = cover.get((r, half), 0) + w
-                if cover[(r, half)] == 512 and cover.get((r ^ 1, half), 0) == 512:
+                cover[r, half] = cover.get((r, half), 0) + w
+                if cover[r, half] == 512 and cover.get((r ^ 1, half), 0) == 512:
                     flips.append((r // 2, half))
 
-        def finish(pair, half, pw):
-            quant_p(pair, half, pw)
-            left[half] -= 1
-            if left[half] == 0:
-                store_scales(half)
+        plan = {1: 3, 2: 4, 3: 5, 4: 6, 5: 7}
+        bcol = keep.tile([P, BLOCKS], BF16, name="bcol")
+        half0, half1, whole = slice(0, 256), slice(256, 512), slice(0, 512)
+        turn(0, 0)
+        turn(0, 1)
+        bank = psum.tile([P, P], BF16, name="rt", bufs=4)
+        nc.tensor.transpose(bank[:], brow[:], identb[:])
+        empty(0, 0, "s")
+        quant_x(0, half0)
+        empty(0, 1, "v")
+        quant_x(0, half1)
+        nc.scalar.copy(out=bcol[:], in_=bank[:, 0:BLOCKS])
+        turn(1, 0)
+        turn(1, 1)
+        project_t(0, 1)
+        project_t(1, 1)
+        empty(1, 0, "s")
+        empty(1, 1, "v")
+        tanh(0)
+        tanh(1)
+        quant_x(1, whole)
+        turn(2, 0)
+        turn(2, 1)
+        lift(0)
+        lift(1)
+        project(0)
+        project(1)
+        project_t(2, 1)
+        project_t(3, 1)
+        empty(2, 0, "s")
+        empty(2, 1, "s")
+        turn(plan[1], 0)
+        turn(plan[1], 1)
 
-        RPAT = "s"
-        PPAT = "s"
-        XPAT = ["s"]
-        for s in range(1, total + 2):
-            if s < total:
-                bias(s)
-            if 1 <= s - 1 < total:
-                square(s - 1)
-            if s < total:
-                tanh(s)
-                if on_g(s):
-                    weigh(s)
-            if s - 1 < total and not on_g(s - 1):
-                weigh(s - 1)
-            if 0 <= s - 2 < total:
-                quant(s - 2)
-            for rect in casts:
-                cast_r(rect, "v")
-                ready(rect)
-            casts = []
-            for n in xwait:
-                quant_x(n)
-            xwait = []
+        todo, made, flipped, planes_q, fresh = [], [], [], [], []
+        quanted = {0, 1}
+        nxt = {"z": 4, "d": 2}
+        count = {"r": 0, "p": 0}
+        RP, PP = "s", "v"
+
+        def more_z(zmax):
+            while nxt["z"] < min(total, zmax) and 2 * chunks[nxt["z"]][0] in quanted:
+                c = nxt["z"]
+                project_t(c, 1 if c < 16 else 1)
+                nxt["z"] += 1
+
+        def more_d(dmax):
+            while nxt["d"] < min(total, dmax) and 2 * chunks[nxt["d"]][0] + 1 in quanted:
+                project(nxt["d"])
+                nxt["d"] += 1
+
+        def some_evac(n):
+            for k in range(n):
+                if flipped:
+                    pair, half, bank = flipped.pop(0)
+                    new_p.append((pair, half, plane(bank, PP[count["p"] % len(PP)])))
+                    count["p"] += 1
+                elif made:
+                    rect, bank = made.pop(0)
+                    emit_r(rect, bank, RP[count["r"] % len(RP)])
+                    count["r"] += 1
+                    new_r.append(rect)
+
+        for i in range(1, pairs + 1):
+            mine = [c for c in (2 * i, 2 * i + 1) if c < total]
+            last = [2 * i - 2, 2 * i - 1]
+            new_p, new_r = [], []
+            weigh(last[0])
+            square(last[1])
+            weigh(last[1])
+            square(last[0])
+            for n in [2] if i == 1 else [plan[i - 1]] if i - 1 in plan else []:
+                quant_x(n, whole)
+                quanted.add(n)
+            some_evac(0)
+            for c in mine:
+                tanh(c)
+            if i in plan:
+                empty(plan[i], 0, "s")
+                empty(plan[i], 1, "s")
+            more_d(2 * i)
+            for c in last:
+                lie(c)
+            some_evac(9)
             for args in planes_q:
                 finish(*args)
-            planes_q = []
-            if 0 <= s - 1 < total:
-                lie(s - 1)
-            for n, h in plan.get(s, []):
-                empty(n, h, XPAT[(2 * n + h) % len(XPAT)])
-                if h == 1:
-                    xwait.append(n)
-            for pair, half, bank in flipped:
-                planes_q.append((pair, half, plane(pair, half, bank, PPAT[count["p"] % len(PPAT)])))
-                count["p"] += 1
-            flipped = []
-            for rect, bank in made:
-                emit_r(rect, bank, RPAT[count["r"] % len(RPAT)])
-                count["r"] += 1
-                casts.append(rect)
-            made = []
-            if s + 1 < total:
-                stage1z(s + 1)
-            if s < total:
-                stage1d(s)
-            for n, h in plan.get(s + 1, []):
-                turn(n, h)
-            if s - 2 in ends[:-1]:
-                lo, hi = PHASES[ends.index(s - 2)]
-                todo.extend(rects(lo, hi))
-            g = s - 2 - (total - GROUPS)
-            for k in range(1):
-                if todo and g < 0:
-                    rect = todo.pop(0)
-                    made.append((rect, stage2(rect, "rt", 4)))
-            if flips and not made[1:]:
-                pair, half = flips.pop(0)
-                flipped.append((pair, half, turn_r(pair, half, "rt", 4)))
-            if 0 <= g:
-                if g == 0:
-                    late = [psum.tile([P, 512], F32, name="rt", bufs=4) for half in range(2)]
-                for half in range(2):
-                    late_pass(late[half], half, g)
+            planes_q = new_p
+            for rect in fresh:
+                if "g" == "v":
+                    cast_r(rect, "v")
+                ready(rect)
+            fresh = new_r
+            for c in last:
+                quant(lc, lsc, l16s, c)
+            for c in last:
+                quant(ac, asc, a16s, c)
+            for rect in new_r:
+                if "g" == "g":
+                    cast_r(rect, "g")
+            for c in mine:
+                lift(c)
+            more_d(2 * i + 2)
+            more_z(2 * i + 4)
+            if i + 1 in plan:
+                turn(plan[i + 1], 0)
+                turn(plan[i + 1], 1)
+            for e, (lo, hi) in zip(ends[:-1], SPANS[:-1]):
+                if e // 2 == i - 1:
+                    todo.extend(rects(lo, hi))
+            for k in range(2):
                 if todo:
                     rect = todo.pop(0)
                     made.append((rect, stage2(rect, "rt", 4)))
+            for k in range(2):
+                if flips and len(made) + len(flipped) < 4:
+                    pair, half = flips.pop(0)
+                    flipped.append((pair, half, turn_r(pair, half, "rt", 4)))
 
         row = BLOCKS - 1
         late_rects = [(row, 1, 512, 512), (row, 1, 0, 512)]
-        ra, rb = rects(last_lo, BLOCKS)[:2]
-        for g in range(total + 2 - 2 - (total - GROUPS), GROUPS):
-            for half in range(2):
-                late_pass(late[half], half, g)
-        ba = stage2(ra, "z", 2)
-        bb = stage2(rb, "z", 2)
-        emit_r(late_rects[1], late[0], "s")
-        emit_r(late_rects[0], late[1], "v")
-        for rect in casts:
-            cast_r(rect, "v")
-            ready(rect)
-        cast_r(late_rects[1], "g")
-        cast_r(late_rects[0], "v")
+        ra, rb = rects(row, BLOCKS)[:2]
+        rest = [ra, rb] + late_rects if 0 else late_rects + [ra, rb]
+        tags = ["d", "d", "z", "z"]
+        tbanks = [stage2(rect, tag, 2) for rect, tag in zip(rest, tags)]
         for args in planes_q:
             finish(*args)
         for pair, half, bank in flipped:
-            finish(pair, half, plane(pair, half, bank, "v"))
+            finish(pair, half, plane(bank, "v"))
+        for rect in fresh:
+            if "g" == "v":
+                cast_r(rect, "v")
+            ready(rect)
         for rect, bank in made:
             emit_r(rect, bank, "s")
             cast_r(rect, "v")
@@ -493,20 +447,14 @@ def tile_generatoredmdstiffnessmatrix_x2_kernel(tc, x, f, w_words, w_scales, b, 
             emit_r(rect, bank, "s")
             cast_r(rect, "v")
             ready(rect)
-        emit_r(ra, ba, "s")
-        cast_r(ra, "v")
-        ready(ra)
-        ready(late_rects[1])
-        emit_r(rb, bb, "v")
-        cast_r(rb, "v")
-        ready(late_rects[0])
-        ready(rb)
+        for n, (rect, bank) in enumerate(zip(rest, tbanks)):
+            emit_r(rect, bank, "svsv"[n])
+            cast_r(rect, "gvvv"[n])
+            ready(rect)
         queue = []
-        n = 0
-        for pair, half in flips:
+        for n, (pair, half) in enumerate(flips):
             bank = turn_r(pair, half, "d" if n % 2 else "rt", 2 if n % 2 else 4)
-            queue.append((pair, half, plane(pair, half, bank, "sv"[n % 2])))
-            n += 1
+            queue.append((pair, half, plane(bank, "sv"[n % 2])))
             if len(queue) > 1:
                 finish(*queue.pop(0))
         for args in queue:

@@ -15,447 +15,413 @@ ALU = mybir.AluOpType
 ACT = mybir.ActivationFunctionType
 
 P = 128
-SAMPLES, FEATS, DICT = 2048, 512, 1024
-GROUPS = SAMPLES // 512
-BLOCKS = DICT // P
-FLOPS = 2 * 2 * SAMPLES * FEATS * DICT + 2 * SAMPLES * DICT * DICT
-NEG_SCALE = -1.0 / math.sqrt(SAMPLES)
+PACK = 4
+GROUP = P * PACK
+SAMPLES, FEATURES, COLUMNS = 2048, 512, 1024
+GROUPS = SAMPLES // GROUP
+BLOCKS = COLUMNS // P
+BANK = 512
+FLOPS = 2 * 2 * SAMPLES * FEATURES * COLUMNS + 2 * SAMPLES * COLUMNS * COLUMNS
+RESULT_SCALE = -1.0 / math.sqrt(SAMPLES)
+
 SPANS = [(0, 4), (4, 5), (5, 6), (6, 7), (7, 8)]
+CHUNKS = [(g, k) for lo, hi in SPANS for g in range(GROUPS) for k in range(lo, hi)]
+PAIRS = len(CHUNKS) // 2
+LAST = BLOCKS - 1
 
 
-def widths(total):
-    parts = []
-    for w in (512, 256, 128):
-        while total >= w:
-            parts.append(w)
-            total -= w
-    return parts
-
-
-def rects(lo, hi):
+def new_rectangles(lo, hi):
     found = []
-    w = (hi - lo) * P
-    per = 512 // w
-    for i in range(0, lo, per):
-        found.append((i, min(per, lo - i), lo * P, w))
+    width = (hi - lo) * P
+    step = BANK // width
+    for i in range(0, lo, step):
+        found.append((i, min(step, lo - i), lo * P, width))
     for half in (1, 0):
-        w = min(hi * P, 512 * (half + 1)) - 512 * half
-        if w <= 0:
-            continue
-        per = max(1, 512 // w)
-        for i in range(lo, hi, per):
-            found.append((i, min(per, hi - i), 512 * half, w))
+        width = min(hi * P, BANK * (half + 1)) - BANK * half
+        if width > 0:
+            for i in range(lo, hi):
+                found.append((i, 1, BANK * half, width))
     return found
+
+
+def pass_widths(columns):
+    parts = []
+    for width in (512, 256, 128):
+        if columns >= width:
+            parts.append(width)
+            columns -= width
+    return parts
 
 
 def tile_generatoredmdstiffnessmatrix_x2_kernel(tc, x, f, w_words, w_scales, b, q, out_0, out_1, out_2):
     nc = tc.nc
     with ExitStack() as ctx:
         keep = ctx.enter_context(tc.tile_pool(name="keep", bufs=1))
-        loads = ctx.enter_context(tc.tile_pool(name="loads", bufs=8))
+        loads = ctx.enter_context(tc.tile_pool(name="loads", bufs=2 * GROUPS))
         work = ctx.enter_context(tc.tile_pool(name="work", bufs=4))
         psum = ctx.enter_context(tc.psum_pool(name="psum", bufs=2))
+
         ctx.enter_context(tc.manual_schedule())
 
-        warm = keep.tile([P, 1], F32, name="warm")
-        nc.vector.memset(warm[:], 0.0)
-        nc.scalar.activation(out=warm[:], in_=warm[:], func=ACT.Tanh)
-        xc = keep.tile([P, 2 * GROUPS, 512], U32, name="xc", align_bytes=64)
-        xs = keep.tile([P, 2 * GROUPS, 512], U8, name="xs", align_bytes=64)
-        brow = keep.tile([P, P], BF16, name="brow")
-        nc.vector.memset(brow[:], 0.0)
-        ws = keep.tile([P, DICT], U8, name="ws", align_bytes=64)
-        nc.vector.memset(ws[:].bitcast(I32), 0)
-        ident = keep.tile([P, P], F32, name="ident")
-        make_identity(nc, ident[:])
-        identb = keep.tile([P, P], BF16, name="identb")
-        nc.vector.tensor_copy(out=identb[:], in_=ident[:])
+        zero = keep.tile([P, 1], F32, name="zero")
+        nc.vector.memset(zero[:], 0.0)
+        bias_rows = keep.tile([P, P], BF16, name="bias_rows")
+        nc.scalar.activation(out=bias_rows[:], in_=zero[:].to_broadcast([P, P]), func=ACT.Tanh)
+        nc.scalar.dma_start(out=bias_rows[0:BLOCKS, :], in_=b.rearrange("(k n) -> k n", n=P))
 
-        wt = keep.tile([P, 2 * DICT], U8, name="wt", align_bytes=64)
-        qt = keep.tile([P, GROUPS * 4], BF16, name="qt")
+        w_scale = keep.tile([P, COLUMNS], U8, name="w_scale", align_bytes=64)
+        nc.vector.memset(w_scale[:].bitcast(I32), 0)
+        identity = keep.tile([P, P], F32, name="identity")
+        make_identity(nc, identity[:])
+        identity_bf16 = keep.tile([P, P], BF16, name="identity_bf16")
+        nc.vector.tensor_copy(out=identity_bf16[:], in_=identity[:])
+
+        w_code = keep.tile([P, 2 * COLUMNS], U8, name="w_code", align_bytes=64)
+        q_bf16 = keep.tile([P, GROUPS, PACK], BF16, name="q_bf16")
         raw = []
-        items = [(src, g) for g in range(GROUPS) for src in (x, f)]
-        for n, (src, g) in enumerate(items):
-            r = loads.tile([P, 4, FEATS], BF16, name="r", align_bytes=64)
-            view = src[512 * g : 512 * (g + 1), :].rearrange("(m t) k -> m t k", t=4)
-            if n < 2:
-                for h in range(2):
-                    nc.sync.dma_start(out=r[:, 2 * h : 2 * h + 2, :], in_=view[:, 2 * h : 2 * h + 2, :])
-            else:
-                nc.sync.dma_start(out=r[:], in_=view)
-            raw.append(r)
+        for n in range(2 * GROUPS):
+            source = (x, f)[n % 2]
+            tile = loads.tile([P, PACK, FEATURES], BF16, name="raw", align_bytes=64)
+            rows = source[GROUP * (n // 2) : GROUP * (n // 2 + 1), :].rearrange("(m t) k -> m t k", t=PACK)
+            step = PACK // 2 if n < 2 else PACK
+            for t in range(0, PACK, step):
+                nc.sync.dma_start(out=tile[:, t : t + step, :], in_=rows[:, t : t + step, :])
+            raw.append(tile)
             if n == 0:
-                nc.sync.dma_start(out=brow[0:BLOCKS, :], in_=b.rearrange("(k n) -> k n", n=P))
-                for quad in range(4):
+                for quadrant in range(4):
                     nc.sync.dma_start(
-                        out=ws[32 * quad : 32 * quad + 4, :].bitcast(I32),
-                        in_=w_scales[0, 4 * quad : 4 * quad + 4, :].bitcast(I32),
+                        out=w_scale[32 * quadrant : 32 * quadrant + 4, :].bitcast(I32),
+                        in_=w_scales[0, 4 * quadrant : 4 * quadrant + 4, :].bitcast(I32),
                     )
-                nc.sync.dma_start(out=wt[:].bitcast(I32), in_=w_words[0].bitcast(I32))
             if n == 1:
-                nc.sync.dma_start(
-                    out=qt[:].rearrange("p (g t) -> p g t", t=4), in_=q.rearrange("(g p t) -> p g t", p=P, t=4)
-                )
+                nc.sync.dma_start(out=w_code[:].bitcast(I32), in_=w_words[0].bitcast(I32))
+                nc.sync.dma_start(out=q_bf16[:], in_=q.rearrange("(g p t) -> p g t", p=P, t=PACK))
 
-        ac = keep.tile([P, GROUPS, DICT], U32, name="ac", align_bytes=64)
-        asc = keep.tile([P, GROUPS, DICT], U8, name="asc", align_bytes=64)
-        lc = keep.tile([P, GROUPS, DICT], U32, name="lc", align_bytes=64)
-        lsc = keep.tile([P, GROUPS, DICT], U8, name="lsc", align_bytes=64)
-        r32 = keep.tile([P, BLOCKS, DICT], F32, name="r32", align_bytes=64)
-        r16 = keep.tile([P, BLOCKS, DICT], BF16, name="r16", align_bytes=64)
-        pc = keep.tile([P, 2, DICT], U32, name="pc", align_bytes=64)
-        psc = keep.tile([P, 2, DICT], U8, name="psc", align_bytes=64)
+        in_code = keep.tile([P, 2 * GROUPS, GROUP], U32, name="in_code", align_bytes=64)
+        in_scale = keep.tile([P, 2 * GROUPS, GROUP], U8, name="in_scale", align_bytes=64)
+        a_code = keep.tile([P, GROUPS, COLUMNS], U32, name="a_code", align_bytes=64)
+        a_scale = keep.tile([P, GROUPS, COLUMNS], U8, name="a_scale", align_bytes=64)
+        l_code = keep.tile([P, GROUPS, COLUMNS], U32, name="l_code", align_bytes=64)
+        l_scale = keep.tile([P, GROUPS, COLUMNS], U8, name="l_scale", align_bytes=64)
+        r_f32 = keep.tile([P, BLOCKS, COLUMNS], F32, name="r_f32", align_bytes=64)
+        r_bf16 = keep.tile([P, BLOCKS, 2, 2, BANK // 2], BF16, name="r_bf16", align_bytes=64)
+        out_code = keep.tile([P, 2, COLUMNS], U32, name="out_code", align_bytes=64)
+        out_scale = keep.tile([P, 2, COLUMNS], U8, name="out_scale", align_bytes=64)
 
-        banks, grouped = {}, {}
+        bias = keep.tile([P, BLOCKS], BF16, name="bias")
 
-        def pull(engine, dst, src):
-            if engine == "s":
-                nc.scalar.copy(out=dst, in_=src)
+        def copy_out(engine, out, in_):
+            if engine == "scalar":
+                nc.scalar.copy(out=out, in_=in_)
             else:
-                nc.vector.tensor_copy(out=dst, in_=src)
+                nc.vector.tensor_copy(out=out, in_=in_)
 
-        def turn(n, h):
+        turned, grouped = {}, {}
+
+        def turn_input(n, h):
             words = raw[n][:].rearrange("m t k -> m (t k)").bitcast(F32)
-            bank = psum.tile([P, 2, 2, P], F32, name="rt", bufs=4)
+            bank = psum.tile([P, 2, 2, P], F32, name="turn", bufs=4)
             for t in range(2):
+                start = FEATURES // 2 * (2 * h + t)
                 for u in range(2):
-                    base = 256 * (2 * h + t)
-                    nc.tensor.transpose(bank[:, t, u, :], words[:, base + u : base + 256 : 2], ident[:])
-            banks[n, h] = bank
+                    nc.tensor.transpose(bank[:, t, u, :], words[:, start + u : start + FEATURES // 2 : 2], identity[:])
+            turned[n, h] = bank
 
-        def empty(n, h, engine):
+        def group_input(n, h, engine):
             if h == 0:
-                xw = work.tile([P, 2048], BF16, name="xw", align_bytes=64, bufs=3)
-                grouped[n] = xw
-            dst = grouped[n][:, 1024 * h : 1024 * (h + 1)].bitcast(F32).rearrange("p (t m u) -> p t m u", t=2, u=2)
-            pull(engine, dst, banks[n, h][:].rearrange("p t u m -> p t m u"))
-
-        def quant_x(n, cols):
-            nc.vector.quantize_mx(
-                out=xc[:, n, cols].bitcast(E4M3),
-                scales=xs[:, n, cols],
-                in_=grouped[n][:, 4 * cols.start : 4 * cols.stop],
+                grouped[n] = work.tile([P, PACK * GROUP], BF16, name="grouped", align_bytes=64, bufs=3)
+            half = grouped[n][:, 1024 * h : 1024 * (h + 1)]
+            copy_out(
+                engine,
+                half.bitcast(F32).rearrange("p (t m u) -> p t m u", t=2, u=2),
+                turned[n, h][:].rearrange("p t u m -> p t m u"),
             )
 
-        chunks = [(g, k) for lo, hi in SPANS for g in range(GROUPS) for k in range(lo, hi)]
-        total = len(chunks)
-        pairs = total // 2
-        ends = [hi * GROUPS - 1 for lo, hi in SPANS]
-        zs, ds, psis, lifted, sqs, a16s, l16s = {}, {}, {}, {}, {}, {}, {}
+        def quantise_input(n, columns):
+            nc.vector.quantize_mx(
+                out=in_code[:, n, columns].bitcast(E4M3),
+                scales=in_scale[:, n, columns],
+                in_=grouped[n][:, PACK * columns.start : PACK * columns.stop],
+            )
 
-        def project_t(c, times):
-            g, k = chunks[c]
-            zt = psum.tile([P, 512], F32, name="z")
-            for r in range(times):
-                nc.tensor.matmul_mx(
-                    out=zt[:],
-                    lhsT=wt[:, 2 * P * k : 2 * P * (k + 1)].bitcast(E2M1),
-                    lhsT_scale=ws[:, P * k : P * (k + 1)],
-                    rhs=xc[:, 2 * g, :].bitcast(E4M3),
-                    rhs_scale=xs[:, 2 * g, :],
-                    start=True,
-                    stop=True,
-                )
-            zs[c] = zt
+        z_bank, d_bank, psi_turned, psi_bank, squares, weighted, derived = {}, {}, {}, {}, {}, {}, {}
 
-        def project(c):
-            g, k = chunks[c]
+        def project_x(c):
+            g, k = CHUNKS[c]
+            z_bank[c] = psum.tile([P, BANK], F32, name="z")
+            nc.tensor.matmul_mx(
+                out=z_bank[c][:],
+                lhsT=w_code[:, 2 * P * k : 2 * P * (k + 1)].bitcast(E2M1),
+                lhsT_scale=w_scale[:, P * k : P * (k + 1)],
+                rhs=in_code[:, 2 * g, :].bitcast(E4M3),
+                rhs_scale=in_scale[:, 2 * g, :],
+                start=True,
+                stop=True,
+            )
+
+        def project_f(c):
+            g, k = CHUNKS[c]
             n = 2 * g + 1
-            d = psum.tile([P, 4, P], F32, name="d")
-            for t in range(4):
+            d_bank[c] = psum.tile([P, PACK, P], F32, name="d")
+            for t in range(PACK):
                 nc.tensor.matmul_mx(
-                    out=d[:, t, :],
-                    lhsT=xc[:, n, P * t : P * (t + 1)].bitcast(E4M3),
-                    lhsT_scale=xs[:, n, P * t : P * (t + 1)],
-                    rhs=wt[:, 2 * P * k : 2 * P * (k + 1)].bitcast(E2M1),
-                    rhs_scale=ws[:, P * k : P * (k + 1)],
+                    out=d_bank[c][:, t, :],
+                    lhsT=in_code[:, n, P * t : P * (t + 1)].bitcast(E4M3),
+                    lhsT_scale=in_scale[:, n, P * t : P * (t + 1)],
+                    rhs=w_code[:, 2 * P * k : 2 * P * (k + 1)].bitcast(E2M1),
+                    rhs_scale=w_scale[:, P * k : P * (k + 1)],
                     start=True,
                     stop=True,
                 )
-            ds[c] = d
 
         def tanh(c):
-            g, k = chunks[c]
-            psi = work.tile([P, 512], F32, name="psi", bufs=4)
-            nc.scalar.activation(out=psi[:], in_=zs[c][:], func=ACT.Tanh, bias=bcol[:, k : k + 1])
-            psis[c] = psi
+            g, k = CHUNKS[c]
+            psi_turned[c] = work.tile([P, BANK], F32, name="psi_turned")
+            nc.scalar.activation(out=psi_turned[c][:], in_=z_bank[c][:], func=ACT.Tanh, bias=bias[:, k : k + 1])
 
-        def lift(c):
-            bank = psum.tile([P, 4, P], F32, name="rt", bufs=4)
-            for t in range(4):
-                nc.tensor.transpose(bank[:, t, :], psis[c][:, P * t : P * (t + 1)], ident[:])
-            lifted[c] = bank
+        def turn_psi(c):
+            psi_bank[c] = psum.tile([P, PACK, P], F32, name="turn", bufs=4)
+            for t in range(PACK):
+                nc.tensor.transpose(psi_bank[c][:, t, :], psi_turned[c][:, P * t : P * (t + 1)], identity[:])
 
-        def inner(tile):
-            return tile[:].rearrange("p (n t) -> p n t", t=4)
-
-        def square(c):
-            sq = work.tile([P, 512], F32, name="sq", bufs=4)
-            nc.scalar.activation(out=inner(sq), in_=lifted[c][:].rearrange("p t n -> p n t"), func=ACT.Square)
-            sqs[c] = sq
+        def half_of(tiles, c, name):
+            if c // 2 not in tiles:
+                tiles[c // 2] = work.tile([P, 2 * PACK * P], BF16, name=name, align_bytes=64)
+            return tiles[c // 2][:, PACK * P * (c % 2) : PACK * P * (c % 2 + 1)]
 
         def weigh(c):
-            g, k = chunks[c]
-            a16 = work.tile([P, 512], BF16, name="a16", align_bytes=64)
+            g, k = CHUNKS[c]
+            factor = q_bf16[:, g, :].unsqueeze(1).unsqueeze(3)
             nc.vector.tensor_tensor(
-                out=inner(a16),
-                in0=lifted[c][:].rearrange("p t n -> p n t"),
-                in1=qt[:, 4 * g : 4 * (g + 1)].unsqueeze(1).to_broadcast([P, P, 4]),
+                out=half_of(weighted, c, "weighted").rearrange("p (c i t) -> p c t i", t=PACK, i=4),
+                in0=psi_bank[c][:].rearrange("p t (c i) -> p c t i", i=4),
+                in1=factor.to_broadcast([P, P // 4, PACK, 4]),
                 op=ALU.mult,
             )
-            a16s[c] = a16
 
-        def lie(c):
-            l16 = work.tile([P, 512], BF16, name="l16", align_bytes=64)
+        def square(c):
+            squares[c] = work.tile([P, PACK * P], F32, name="squares")
+            nc.scalar.activation(
+                out=squares[c][:].rearrange("p (n t) -> p n t", t=PACK),
+                in_=psi_bank[c][:].rearrange("p t n -> p n t"),
+                func=ACT.Square,
+            )
+
+        def derive(c):
             nc.vector.scalar_tensor_tensor(
-                out=inner(l16),
-                in0=inner(sqs[c]),
+                out=half_of(derived, c, "derived").rearrange("p (n t) -> p n t", t=PACK),
+                in0=squares[c][:].rearrange("p (n t) -> p n t", t=PACK),
                 scalar=1.0,
-                in1=ds[c][:].rearrange("p t n -> p n t"),
+                in1=d_bank[c][:].rearrange("p t n -> p n t"),
                 op0=ALU.subtract,
                 op1=ALU.mult,
             )
-            l16s[c] = l16
 
-        def quant(codes, scales, src, c):
-            g, k = chunks[c]
-            cols = slice(P * k, P * (k + 1))
-            nc.vector.quantize_mx(out=codes[:, g, cols].bitcast(E4M3), scales=scales[:, g, cols], in_=src[c][:])
+        def quantise_pair(code, scale, values, c):
+            (g, k), (g_next, k_next) = CHUNKS[c], CHUNKS[c + 1]
+            if g == g_next:
+                parts = [(g, slice(P * k, P * (k + 2)), slice(0, 2 * PACK * P))]
+            else:
+                parts = [
+                    (g, slice(P * k, P * (k + 1)), slice(0, PACK * P)),
+                    (g_next, slice(P * k_next, P * (k_next + 1)), slice(PACK * P, 2 * PACK * P)),
+                ]
+            for group, columns, part in parts:
+                nc.vector.quantize_mx(
+                    out=code[:, group, columns].bitcast(E4M3), scales=scale[:, group, columns], in_=values[c // 2][:, part]
+                )
 
-        def gram(bank, col, i, j0, n, g):
+        def add_group(out, row, column, g):
+            columns = slice(column, column + out.shape[1])
             nc.tensor.matmul_mx(
-                out=bank[:, col : col + n],
-                lhsT=ac[:, g, P * i : P * (i + 1)].bitcast(E4M3),
-                lhsT_scale=asc[:, g, P * i : P * (i + 1)],
-                rhs=lc[:, g, j0 : j0 + n].bitcast(E4M3),
-                rhs_scale=lsc[:, g, j0 : j0 + n],
+                out=out,
+                lhsT=a_code[:, g, P * row : P * (row + 1)].bitcast(E4M3),
+                lhsT_scale=a_scale[:, g, P * row : P * (row + 1)],
+                rhs=l_code[:, g, columns].bitcast(E4M3),
+                rhs_scale=l_scale[:, g, columns],
                 start=(g == 0),
                 stop=(g == GROUPS - 1),
             )
 
-        def stage2(rect, tag, bufs):
-            i0, rows, j0, w = rect
-            bank = psum.tile([P, 512], F32, name=tag, bufs=bufs)
+        def multiply(rectangle, name, bufs):
+            row, rows, column, width = rectangle
+            bank = psum.tile([P, BANK], F32, name=name, bufs=bufs)
             for r in range(rows):
-                col = 0
-                for n in widths(w):
+                done = 0
+                for n in pass_widths(width):
                     for g in range(GROUPS):
-                        gram(bank, r * w + col, i0 + r, j0 + col, n, g)
-                    col += n
+                        add_group(bank[:, r * width + done : r * width + done + n], row + r, column + done, g)
+                    done += n
             return bank
 
-        def emit_r(rect, bank, engine):
-            i0, rows, j0, w = rect
-            dst = r32[:, i0 : i0 + rows, j0 : j0 + w]
-            src = bank[:, 0 : rows * w].rearrange("p (r w) -> p r w", r=rows)
-            if engine == "s":
-                nc.scalar.activation(out=dst, in_=src, func=ACT.Copy, scale=NEG_SCALE)
+        def scale_and_store(rectangle, bank, engine):
+            row, rows, column, width = rectangle
+            out = r_f32[:, row : row + rows, column : column + width]
+            in_ = bank[:, 0 : rows * width].rearrange("p (r n) -> p r n", r=rows)
+            if engine == "scalar":
+                nc.scalar.activation(out=out, in_=in_, func=ACT.Copy, scale=RESULT_SCALE)
             else:
-                nc.vector.tensor_scalar(out=dst, in0=src, scalar1=NEG_SCALE, scalar2=None, op0=ALU.mult)
-            for r in range(i0, i0 + rows):
-                nc.sync.dma_start(out=out_0[P * r : P * (r + 1), j0 : j0 + w], in_=r32[:, r, j0 : j0 + w])
+                nc.vector.tensor_scalar(out=out, in0=in_, scalar1=RESULT_SCALE, scalar2=None, op0=ALU.mult)
+            for r in range(row, row + rows):
+                nc.sync.dma_start(
+                    out=out_0[P * r : P * (r + 1), column : column + width], in_=r_f32[:, r, column : column + width]
+                )
 
-        def cast_r(rect, engine):
-            i0, rows, j0, w = rect
-            src = r32[:, i0 : i0 + rows, j0 : j0 + w]
-            dst = r16[:, i0 : i0 + rows, j0 : j0 + w]
-            if engine == "g":
-                nc.gpsimd.tensor_scalar(out=dst, in0=src, scalar1=1.0, scalar2=1.0, op0=ALU.mult, op1=ALU.mult)
-            else:
-                nc.vector.tensor_copy(out=dst, in_=src)
+        def round_result(rectangle, engine):
+            row, rows, column, width = rectangle
+            half, start = column // BANK, column % BANK // 2
+            pairs = r_f32[:, row : row + rows, column : column + width].rearrange("p r (n u e) -> p r u n e", u=2, e=2)
+            for u in range(2):
+                out = r_bf16[:, row : row + rows, half, u, start : start + width // 2]
+                out = out.rearrange("p r (n e) -> p r n e", e=2)
+                if engine == "gpsimd":
+                    nc.gpsimd.tensor_scalar(
+                        out=out, in0=pairs[:, :, u, :, :], scalar1=1.0, scalar2=1.0, op0=ALU.mult, op1=ALU.mult
+                    )
+                else:
+                    nc.vector.tensor_copy(out=out, in_=pairs[:, :, u, :, :])
 
-        def turn_r(pair, half, tag, bufs):
-            bank = psum.tile([P, 2, 2, P], F32, name=tag, bufs=bufs)
+        covered = {}
+
+        def newly_complete(rectangle):
+            row, rows, column, width = rectangle
+            half = column // BANK
+            complete = []
+            for r in range(row, row + rows):
+                covered[r, half] = covered.get((r, half), 0) + width
+                if covered[r, half] == BANK and covered.get((r // 2 * 2 + 1 - r % 2, half), 0) == BANK:
+                    complete.append((r // 2, half))
+            return complete
+
+        def turn_result(pair, half, name, bufs):
+            bank = psum.tile([P, 2, 2, P], F32, name=name, bufs=bufs)
             for e in range(2):
-                words = r16[:, 2 * pair + e, 512 * half : 512 * (half + 1)].bitcast(F32)
                 for u in range(2):
-                    nc.tensor.transpose(bank[:, e, u, :], words[:, u:256:2], ident[:])
+                    nc.tensor.transpose(bank[:, e, u, :], r_bf16[:, 2 * pair + e, half, u, :].bitcast(F32), identity[:])
             return bank
 
-        def plane(bank, engine):
-            pw = work.tile([P, 1024], BF16, name="pw", align_bytes=64)
-            dst = pw[:].bitcast(F32).rearrange("p (e m u) -> p e m u", e=2, u=2)
-            pull(engine, dst, bank[:].rearrange("p e u m -> p e m u"))
-            return pw
-
-        left = {0: 4, 1: 4}
-
-        def finish(pair, half, pw):
-            cols = slice(256 * pair, 256 * (pair + 1))
-            nc.vector.quantize_mx(out=pc[:, half, cols].bitcast(E4M3), scales=psc[:, half, cols], in_=pw[:])
-            nc.sync.dma_start(
-                out=out_1[half, :, cols, :].rearrange("p m t -> p (m t)").bitcast(I32),
-                in_=pc[:, half, cols].bitcast(I32),
+        def group_result(bank, engine):
+            tile = work.tile([P, 2 * PACK * P], BF16, name="grouped_result", align_bytes=64)
+            copy_out(
+                engine,
+                tile[:].bitcast(F32).rearrange("p (e m u) -> p e m u", e=2, u=2),
+                bank[:].rearrange("p e u m -> p e m u"),
             )
-            left[half] -= 1
-            if left[half] == 0:
-                for quad in range(4):
+            return tile
+
+        planes_left = [BLOCKS // 2, BLOCKS // 2]
+
+        def quantise_and_store(pair, half, tile):
+            columns = slice(2 * P * pair, 2 * P * (pair + 1))
+            nc.vector.quantize_mx(
+                out=out_code[:, half, columns].bitcast(E4M3), scales=out_scale[:, half, columns], in_=tile[:]
+            )
+            nc.sync.dma_start(
+                out=out_1[half, :, columns, :].rearrange("p m t -> p (m t)").bitcast(I32),
+                in_=out_code[:, half, columns].bitcast(I32),
+            )
+            planes_left[half] -= 1
+            if planes_left[half] == 0:
+                for quadrant in range(4):
                     nc.sync.dma_start(
-                        out=out_2[half, 4 * quad : 4 * quad + 4, :].bitcast(I32),
-                        in_=psc[32 * quad : 32 * quad + 4, half, :].bitcast(I32),
+                        out=out_2[half, 4 * quadrant : 4 * quadrant + 4, :].bitcast(I32),
+                        in_=out_scale[32 * quadrant : 32 * quadrant + 4, half, :].bitcast(I32),
                     )
 
-        flips, cover = [], {}
+        turn_input(0, 0)
+        turn_input(0, 1)
+        bias_bank = psum.tile([P, P], BF16, name="turn", bufs=4)
+        nc.tensor.transpose(bias_bank[:], bias_rows[:], identity_bf16[:])
+        group_input(0, 0, "scalar")
+        group_input(0, 1, "vector")
+        quantise_input(0, slice(0, GROUP // 2))
+        quantise_input(0, slice(GROUP // 2, GROUP))
+        turn_input(1, 0)
+        turn_input(1, 1)
+        project_x(0)
+        project_x(1)
+        group_input(1, 0, "scalar")
+        group_input(1, 1, "vector")
+        nc.scalar.copy(out=bias[:], in_=bias_bank[:, 0:BLOCKS])
+        turn_input(2, 0)
+        turn_input(2, 1)
 
-        def ready(rect):
-            i0, rows, j0, w = rect
-            half = j0 // 512
-            for r in range(i0, i0 + rows):
-                cover[r, half] = cover.get((r, half), 0) + w
-                if cover[r, half] == 512 and cover.get((r ^ 1, half), 0) == 512:
-                    flips.append((r // 2, half))
+        to_multiply, in_psum, rounded, to_turn, in_turn, to_quantise = [], [], [], [], [], []
+        last_rows = [(LAST, 1, BANK * half, BANK) for half in (1, 0)]
+        for i in range(PAIRS + 1):
+            current = [2 * i, 2 * i + 1] if i < PAIRS else []
 
-        plan = {1: 3, 2: 4, 3: 5, 4: 6, 5: 7}
-        bcol = keep.tile([P, BLOCKS], BF16, name="bcol")
-        half0, half1, whole = slice(0, 256), slice(256, 512), slice(0, 512)
-        turn(0, 0)
-        turn(0, 1)
-        bank = psum.tile([P, P], BF16, name="rt", bufs=4)
-        nc.tensor.transpose(bank[:], brow[:], identb[:])
-        empty(0, 0, "s")
-        quant_x(0, half0)
-        empty(0, 1, "v")
-        quant_x(0, half1)
-        nc.scalar.copy(out=bcol[:], in_=bank[:, 0:BLOCKS])
-        turn(1, 0)
-        turn(1, 1)
-        project_t(0, 1)
-        project_t(1, 1)
-        empty(1, 0, "s")
-        empty(1, 1, "v")
-        tanh(0)
-        tanh(1)
-        quant_x(1, whole)
-        turn(2, 0)
-        turn(2, 1)
-        lift(0)
-        lift(1)
-        project(0)
-        project(1)
-        project_t(2, 1)
-        project_t(3, 1)
-        empty(2, 0, "s")
-        empty(2, 1, "s")
-        turn(plan[1], 0)
-        turn(plan[1], 1)
-
-        todo, made, flipped, planes_q, fresh = [], [], [], [], []
-        quanted = {0, 1}
-        nxt = {"z": 4, "d": 2}
-        count = {"r": 0, "p": 0}
-        RP, PP = "s", "v"
-
-        def more_z(zmax):
-            while nxt["z"] < min(total, zmax) and 2 * chunks[nxt["z"]][0] in quanted:
-                c = nxt["z"]
-                project_t(c, 1 if c < 16 else 1)
-                nxt["z"] += 1
-
-        def more_d(dmax):
-            while nxt["d"] < min(total, dmax) and 2 * chunks[nxt["d"]][0] + 1 in quanted:
-                project(nxt["d"])
-                nxt["d"] += 1
-
-        def some_evac(n):
-            for k in range(n):
-                if flipped:
-                    pair, half, bank = flipped.pop(0)
-                    new_p.append((pair, half, plane(bank, PP[count["p"] % len(PP)])))
-                    count["p"] += 1
-                elif made:
-                    rect, bank = made.pop(0)
-                    emit_r(rect, bank, RP[count["r"] % len(RP)])
-                    count["r"] += 1
-                    new_r.append(rect)
-
-        for i in range(1, pairs + 1):
-            mine = [c for c in (2 * i, 2 * i + 1) if c < total]
-            last = [2 * i - 2, 2 * i - 1]
-            new_p, new_r = [], []
-            weigh(last[0])
-            square(last[1])
-            weigh(last[1])
-            square(last[0])
-            for n in [2] if i == 1 else [plan[i - 1]] if i - 1 in plan else []:
-                quant_x(n, whole)
-                quanted.add(n)
-            some_evac(0)
-            for c in mine:
+            if i > 0:
+                first, second = 2 * i - 2, 2 * i - 1
+                weigh(first)
+                square(second)
+            if i + 1 < 2 * GROUPS:
+                quantise_input(i + 1, slice(0, GROUP))
+            if i > 0:
+                weigh(second)
+                square(first)
+            for c in current:
                 tanh(c)
-            if i in plan:
-                empty(plan[i], 0, "s")
-                empty(plan[i], 1, "s")
-            more_d(2 * i)
-            for c in last:
-                lie(c)
-            some_evac(9)
-            for args in planes_q:
-                finish(*args)
-            planes_q = new_p
-            for rect in fresh:
-                if "g" == "v":
-                    cast_r(rect, "v")
-                ready(rect)
-            fresh = new_r
-            for c in last:
-                quant(lc, lsc, l16s, c)
-            for c in last:
-                quant(ac, asc, a16s, c)
-            for rect in new_r:
-                if "g" == "g":
-                    cast_r(rect, "g")
-            for c in mine:
-                lift(c)
-            more_d(2 * i + 2)
-            more_z(2 * i + 4)
-            if i + 1 in plan:
-                turn(plan[i + 1], 0)
-                turn(plan[i + 1], 1)
-            for e, (lo, hi) in zip(ends[:-1], SPANS[:-1]):
-                if e // 2 == i - 1:
-                    todo.extend(rects(lo, hi))
-            for k in range(2):
-                if todo:
-                    rect = todo.pop(0)
-                    made.append((rect, stage2(rect, "rt", 4)))
-            for k in range(2):
-                if flips and len(made) + len(flipped) < 4:
-                    pair, half = flips.pop(0)
-                    flipped.append((pair, half, turn_r(pair, half, "rt", 4)))
+            if i + 2 < 2 * GROUPS:
+                group_input(i + 2, 0, "scalar")
+                group_input(i + 2, 1, "scalar")
+            if i > 0:
+                derive(second)
+                derive(first)
 
-        row = BLOCKS - 1
-        late_rects = [(row, 1, 512, 512), (row, 1, 0, 512)]
-        ra, rb = rects(row, BLOCKS)[:2]
-        rest = [ra, rb] + late_rects if 0 else late_rects + [ra, rb]
-        tags = ["d", "d", "z", "z"]
-        tbanks = [stage2(rect, tag, 2) for rect, tag in zip(rest, tags)]
-        for args in planes_q:
-            finish(*args)
-        for pair, half, bank in flipped:
-            finish(pair, half, plane(bank, "v"))
-        for rect in fresh:
-            if "g" == "v":
-                cast_r(rect, "v")
-            ready(rect)
-        for rect, bank in made:
-            emit_r(rect, bank, "s")
-            cast_r(rect, "v")
-            ready(rect)
-        while todo:
-            rect = todo.pop(0)
-            bank = stage2(rect, "rt", 4)
-            emit_r(rect, bank, "s")
-            cast_r(rect, "v")
-            ready(rect)
-        for n, (rect, bank) in enumerate(zip(rest, tbanks)):
-            emit_r(rect, bank, "svsv"[n])
-            cast_r(rect, "gvvv"[n])
-            ready(rect)
-        queue = []
-        for n, (pair, half) in enumerate(flips):
-            bank = turn_r(pair, half, "d" if n % 2 else "rt", 2 if n % 2 else 4)
-            queue.append((pair, half, plane(bank, "sv"[n % 2])))
-            if len(queue) > 1:
-                finish(*queue.pop(0))
-        for args in queue:
-            finish(*args)
+            grouped_now = [(pair, half, group_result(bank, "scalar")) for pair, half, bank in in_turn]
+            for rectangle, bank in in_psum:
+                scale_and_store(rectangle, bank, "scalar")
+            for pair, half, tile in to_quantise:
+                quantise_and_store(pair, half, tile)
+            to_quantise = grouped_now
+            for rectangle in rounded:
+                to_turn.extend(newly_complete(rectangle))
+            if i > 0:
+                quantise_pair(a_code, a_scale, weighted, first)
+                quantise_pair(l_code, l_scale, derived, first)
+            rounded = [rectangle for rectangle, bank in in_psum]
+            for rectangle in rounded:
+                round_result(rectangle, "gpsimd")
+
+            for c in current:
+                turn_psi(c)
+            for c in current:
+                project_f(c)
+            for c in (2 * i + 2, 2 * i + 3):
+                if c < len(CHUNKS):
+                    project_x(c)
+            if i + 3 < 2 * GROUPS:
+                turn_input(i + 3, 0)
+                turn_input(i + 3, 1)
+            for lo, hi in SPANS[:-1]:
+                if GROUPS * hi == 2 * i:
+                    to_multiply.extend(new_rectangles(lo, hi))
+            in_psum = [(rectangle, multiply(rectangle, "turn", 4)) for rectangle in to_multiply[:2]]
+            to_multiply = to_multiply[2:]
+            in_turn = [(pair, half, turn_result(pair, half, "turn", 4)) for pair, half in to_turn[:1]]
+            to_turn = to_turn[1:]
+
+        last_banks = [psum.tile([P, BANK], F32, name="z") for rectangle in last_rows]
+        for g in range(GROUPS):
+            for rectangle, bank in zip(last_rows, last_banks):
+                add_group(bank[:], LAST, rectangle[2], g)
+        last_columns = new_rectangles(LAST, BLOCKS)[:2]
+        last_banks.extend([multiply(rectangle, "d", 2) for rectangle in last_columns])
+        for pair, half, tile in to_quantise:
+            quantise_and_store(pair, half, tile)
+        for rectangle in rounded:
+            to_turn.extend(newly_complete(rectangle))
+        engines = [("vector", "gpsimd"), ("scalar", "vector"), ("vector", "vector"), ("scalar", "vector")]
+        for rectangle, bank, (store_engine, round_engine) in zip(last_rows + last_columns, last_banks, engines):
+            scale_and_store(rectangle, bank, store_engine)
+            round_result(rectangle, round_engine)
+            to_turn.extend(newly_complete(rectangle))
+
+        for n, (pair, half) in enumerate(to_turn):
+            bank = turn_result(pair, half, "d" if n % 2 else "turn", 2 if n % 2 else 4)
+            tile = group_result(bank, "vector" if n % 2 else "scalar")
+            if n > 0:
+                quantise_and_store(*waiting)
+            waiting = (pair, half, tile)
+        quantise_and_store(*waiting)

import math
from contextlib import ExitStack

import concourse.mybir as mybir
from concourse.masks import make_identity

F32 = mybir.dt.float32
BF16 = mybir.dt.bfloat16
I32 = mybir.dt.int32
U32 = mybir.dt.uint32
U8 = mybir.dt.uint8
E4M3 = mybir.dt.float8_e4m3fn_x4
E2M1 = mybir.dt.float4_e2m1fn_x4
ALU = mybir.AluOpType
ACT = mybir.ActivationFunctionType

P = 128
PACK = 4
GROUP = P * PACK
SAMPLES, FEATURES, COLUMNS = 2048, 512, 1024
GROUPS = SAMPLES // GROUP
BLOCKS = COLUMNS // P
BANK = 512
FLOPS = 2 * 2 * SAMPLES * FEATURES * COLUMNS + 2 * SAMPLES * COLUMNS * COLUMNS
RESULT_SCALE = -1.0 / math.sqrt(SAMPLES)

SPANS = [(0, 4), (4, 5), (5, 6), (6, 7), (7, 8)]
CHUNKS = [(g, k) for lo, hi in SPANS for g in range(GROUPS) for k in range(lo, hi)]
PAIRS = len(CHUNKS) // 2
LAST = BLOCKS - 1


def new_rectangles(lo, hi):
    found = []
    width = (hi - lo) * P
    step = BANK // width
    for i in range(0, lo, step):
        found.append((i, min(step, lo - i), lo * P, width))
    for half in (1, 0):
        width = min(hi * P, BANK * (half + 1)) - BANK * half
        if width > 0:
            for i in range(lo, hi):
                found.append((i, 1, BANK * half, width))
    return found


def pass_widths(columns):
    parts = []
    for width in (512, 256, 128):
        if columns >= width:
            parts.append(width)
            columns -= width
    return parts


def tile_generatoredmdstiffnessmatrix_x2_kernel(tc, x, f, w_words, w_scales, b, q, out_0, out_1, out_2):
    nc = tc.nc
    with ExitStack() as ctx:
        keep = ctx.enter_context(tc.tile_pool(name="keep", bufs=1))
        loads = ctx.enter_context(tc.tile_pool(name="loads", bufs=2 * GROUPS))
        work = ctx.enter_context(tc.tile_pool(name="work", bufs=4))
        psum = ctx.enter_context(tc.psum_pool(name="psum", bufs=2))

        ctx.enter_context(tc.manual_schedule())

        zero = keep.tile([P, 1], F32, name="zero")
        nc.vector.memset(zero[:], 0.0)
        bias_rows = keep.tile([P, P], BF16, name="bias_rows")
        nc.scalar.activation(out=bias_rows[:], in_=zero[:].to_broadcast([P, P]), func=ACT.Tanh)
        nc.scalar.dma_start(out=bias_rows[0:BLOCKS, :], in_=b.rearrange("(k n) -> k n", n=P))

        w_scale = keep.tile([P, COLUMNS], U8, name="w_scale", align_bytes=64)
        nc.vector.memset(w_scale[:].bitcast(I32), 0)
        identity = keep.tile([P, P], F32, name="identity")
        make_identity(nc, identity[:])
        identity_bf16 = keep.tile([P, P], BF16, name="identity_bf16")
        nc.vector.tensor_copy(out=identity_bf16[:], in_=identity[:])

        w_code = keep.tile([P, 2 * COLUMNS], U8, name="w_code", align_bytes=64)
        q_bf16 = keep.tile([P, GROUPS, PACK], BF16, name="q_bf16")
        raw = []
        for n in range(2 * GROUPS):
            source = (x, f)[n % 2]
            tile = loads.tile([P, PACK, FEATURES], BF16, name="raw", align_bytes=64)
            rows = source[GROUP * (n // 2) : GROUP * (n // 2 + 1), :].rearrange("(m t) k -> m t k", t=PACK)
            step = PACK // 2 if n < 2 else PACK
            for t in range(0, PACK, step):
                nc.sync.dma_start(out=tile[:, t : t + step, :], in_=rows[:, t : t + step, :])
            raw.append(tile)
            if n == 0:
                for quadrant in range(4):
                    nc.sync.dma_start(
                        out=w_scale[32 * quadrant : 32 * quadrant + 4, :].bitcast(I32),
                        in_=w_scales[0, 4 * quadrant : 4 * quadrant + 4, :].bitcast(I32),
                    )
            if n == 1:
                nc.sync.dma_start(out=w_code[:].bitcast(I32), in_=w_words[0].bitcast(I32))
                nc.sync.dma_start(out=q_bf16[:], in_=q.rearrange("(g p t) -> p g t", p=P, t=PACK))

        in_code = keep.tile([P, 2 * GROUPS, GROUP], U32, name="in_code", align_bytes=64)
        in_scale = keep.tile([P, 2 * GROUPS, GROUP], U8, name="in_scale", align_bytes=64)
        a_code = keep.tile([P, GROUPS, COLUMNS], U32, name="a_code", align_bytes=64)
        a_scale = keep.tile([P, GROUPS, COLUMNS], U8, name="a_scale", align_bytes=64)
        l_code = keep.tile([P, GROUPS, COLUMNS], U32, name="l_code", align_bytes=64)
        l_scale = keep.tile([P, GROUPS, COLUMNS], U8, name="l_scale", align_bytes=64)
        r_f32 = keep.tile([P, BLOCKS, COLUMNS], F32, name="r_f32", align_bytes=64)
        r_bf16 = keep.tile([P, BLOCKS, 2, 2, BANK // 2], BF16, name="r_bf16", align_bytes=64)
        out_code = keep.tile([P, 2, COLUMNS], U32, name="out_code", align_bytes=64)
        out_scale = keep.tile([P, 2, COLUMNS], U8, name="out_scale", align_bytes=64)

        bias = keep.tile([P, BLOCKS], BF16, name="bias")

        def copy_out(engine, out, in_):
            if engine == "scalar":
                nc.scalar.copy(out=out, in_=in_)
            else:
                nc.vector.tensor_copy(out=out, in_=in_)

        turned, grouped = {}, {}

        def turn_input(n, h):
            words = raw[n][:].rearrange("m t k -> m (t k)").bitcast(F32)
            bank = psum.tile([P, 2, 2, P], F32, name="turn", bufs=4)
            for t in range(2):
                start = FEATURES // 2 * (2 * h + t)
                for u in range(2):
                    nc.tensor.transpose(bank[:, t, u, :], words[:, start + u : start + FEATURES // 2 : 2], identity[:])
            turned[n, h] = bank

        def group_input(n, h, engine):
            if h == 0:
                grouped[n] = work.tile([P, PACK * GROUP], BF16, name="grouped", align_bytes=64, bufs=3)
            half = grouped[n][:, 1024 * h : 1024 * (h + 1)]
            copy_out(
                engine,
                half.bitcast(F32).rearrange("p (t m u) -> p t m u", t=2, u=2),
                turned[n, h][:].rearrange("p t u m -> p t m u"),
            )

        def quantise_input(n, columns):
            nc.vector.quantize_mx(
                out=in_code[:, n, columns].bitcast(E4M3),
                scales=in_scale[:, n, columns],
                in_=grouped[n][:, PACK * columns.start : PACK * columns.stop],
            )

        z_bank, d_bank, psi_turned, psi_bank, squares, weighted, derived = {}, {}, {}, {}, {}, {}, {}

        def project_x(c):
            g, k = CHUNKS[c]
            z_bank[c] = psum.tile([P, BANK], F32, name="z")
            nc.tensor.matmul_mx(
                out=z_bank[c][:],
                lhsT=w_code[:, 2 * P * k : 2 * P * (k + 1)].bitcast(E2M1),
                lhsT_scale=w_scale[:, P * k : P * (k + 1)],
                rhs=in_code[:, 2 * g, :].bitcast(E4M3),
                rhs_scale=in_scale[:, 2 * g, :],
                start=True,
                stop=True,
            )

        def project_f(c):
            g, k = CHUNKS[c]
            n = 2 * g + 1
            d_bank[c] = psum.tile([P, PACK, P], F32, name="d")
            for t in range(PACK):
                nc.tensor.matmul_mx(
                    out=d_bank[c][:, t, :],
                    lhsT=in_code[:, n, P * t : P * (t + 1)].bitcast(E4M3),
                    lhsT_scale=in_scale[:, n, P * t : P * (t + 1)],
                    rhs=w_code[:, 2 * P * k : 2 * P * (k + 1)].bitcast(E2M1),
                    rhs_scale=w_scale[:, P * k : P * (k + 1)],
                    start=True,
                    stop=True,
                )

        def tanh(c):
            g, k = CHUNKS[c]
            psi_turned[c] = work.tile([P, BANK], F32, name="psi_turned")
            nc.scalar.activation(out=psi_turned[c][:], in_=z_bank[c][:], func=ACT.Tanh, bias=bias[:, k : k + 1])

        def turn_psi(c):
            psi_bank[c] = psum.tile([P, PACK, P], F32, name="turn", bufs=4)
            for t in range(PACK):
                nc.tensor.transpose(psi_bank[c][:, t, :], psi_turned[c][:, P * t : P * (t + 1)], identity[:])

        def half_of(tiles, c, name):
            if c // 2 not in tiles:
                tiles[c // 2] = work.tile([P, 2 * PACK * P], BF16, name=name, align_bytes=64)
            return tiles[c // 2][:, PACK * P * (c % 2) : PACK * P * (c % 2 + 1)]

        def weigh(c):
            g, k = CHUNKS[c]
            factor = q_bf16[:, g, :].unsqueeze(1).unsqueeze(3)
            nc.vector.tensor_tensor(
                out=half_of(weighted, c, "weighted").rearrange("p (c i t) -> p c t i", t=PACK, i=4),
                in0=psi_bank[c][:].rearrange("p t (c i) -> p c t i", i=4),
                in1=factor.to_broadcast([P, P // 4, PACK, 4]),
                op=ALU.mult,
            )

        def square(c):
            squares[c] = work.tile([P, PACK * P], F32, name="squares")
            nc.scalar.activation(
                out=squares[c][:].rearrange("p (n t) -> p n t", t=PACK),
                in_=psi_bank[c][:].rearrange("p t n -> p n t"),
                func=ACT.Square,
            )

        def derive(c):
            nc.vector.scalar_tensor_tensor(
                out=half_of(derived, c, "derived").rearrange("p (n t) -> p n t", t=PACK),
                in0=squares[c][:].rearrange("p (n t) -> p n t", t=PACK),
                scalar=1.0,
                in1=d_bank[c][:].rearrange("p t n -> p n t"),
                op0=ALU.subtract,
                op1=ALU.mult,
            )

        def quantise_pair(code, scale, values, c):
            (g, k), (g_next, k_next) = CHUNKS[c], CHUNKS[c + 1]
            if g == g_next:
                parts = [(g, slice(P * k, P * (k + 2)), slice(0, 2 * PACK * P))]
            else:
                parts = [
                    (g, slice(P * k, P * (k + 1)), slice(0, PACK * P)),
                    (g_next, slice(P * k_next, P * (k_next + 1)), slice(PACK * P, 2 * PACK * P)),
                ]
            for group, columns, part in parts:
                nc.vector.quantize_mx(
                    out=code[:, group, columns].bitcast(E4M3), scales=scale[:, group, columns], in_=values[c // 2][:, part]
                )

        def add_group(out, row, column, g):
            columns = slice(column, column + out.shape[1])
            nc.tensor.matmul_mx(
                out=out,
                lhsT=a_code[:, g, P * row : P * (row + 1)].bitcast(E4M3),
                lhsT_scale=a_scale[:, g, P * row : P * (row + 1)],
                rhs=l_code[:, g, columns].bitcast(E4M3),
                rhs_scale=l_scale[:, g, columns],
                start=(g == 0),
                stop=(g == GROUPS - 1),
            )

        def multiply(rectangle, name, bufs):
            row, rows, column, width = rectangle
            bank = psum.tile([P, BANK], F32, name=name, bufs=bufs)
            for r in range(rows):
                done = 0
                for n in pass_widths(width):
                    for g in range(GROUPS):
                        add_group(bank[:, r * width + done : r * width + done + n], row + r, column + done, g)
                    done += n
            return bank

        def scale_and_store(rectangle, bank, engine):
            row, rows, column, width = rectangle
            out = r_f32[:, row : row + rows, column : column + width]
            in_ = bank[:, 0 : rows * width].rearrange("p (r n) -> p r n", r=rows)
            if engine == "scalar":
                nc.scalar.activation(out=out, in_=in_, func=ACT.Copy, scale=RESULT_SCALE)
            else:
                nc.vector.tensor_scalar(out=out, in0=in_, scalar1=RESULT_SCALE, scalar2=None, op0=ALU.mult)
            for r in range(row, row + rows):
                nc.sync.dma_start(
                    out=out_0[P * r : P * (r + 1), column : column + width], in_=r_f32[:, r, column : column + width]
                )

        def round_result(rectangle, engine):
            row, rows, column, width = rectangle
            half, start = column // BANK, column % BANK // 2
            pairs = r_f32[:, row : row + rows, column : column + width].rearrange("p r (n u e) -> p r u n e", u=2, e=2)
            for u in range(2):
                out = r_bf16[:, row : row + rows, half, u, start : start + width // 2]
                out = out.rearrange("p r (n e) -> p r n e", e=2)
                if engine == "gpsimd":
                    nc.gpsimd.tensor_scalar(
                        out=out, in0=pairs[:, :, u, :, :], scalar1=1.0, scalar2=1.0, op0=ALU.mult, op1=ALU.mult
                    )
                else:
                    nc.vector.tensor_copy(out=out, in_=pairs[:, :, u, :, :])

        covered = {}

        def newly_complete(rectangle):
            row, rows, column, width = rectangle
            half = column // BANK
            complete = []
            for r in range(row, row + rows):
                covered[r, half] = covered.get((r, half), 0) + width
                if covered[r, half] == BANK and covered.get((r // 2 * 2 + 1 - r % 2, half), 0) == BANK:
                    complete.append((r // 2, half))
            return complete

        def turn_result(pair, half, name, bufs):
            bank = psum.tile([P, 2, 2, P], F32, name=name, bufs=bufs)
            for e in range(2):
                for u in range(2):
                    nc.tensor.transpose(bank[:, e, u, :], r_bf16[:, 2 * pair + e, half, u, :].bitcast(F32), identity[:])
            return bank

        def group_result(bank, engine):
            tile = work.tile([P, 2 * PACK * P], BF16, name="grouped_result", align_bytes=64)
            copy_out(
                engine,
                tile[:].bitcast(F32).rearrange("p (e m u) -> p e m u", e=2, u=2),
                bank[:].rearrange("p e u m -> p e m u"),
            )
            return tile

        planes_left = [BLOCKS // 2, BLOCKS // 2]

        def quantise_and_store(pair, half, tile):
            columns = slice(2 * P * pair, 2 * P * (pair + 1))
            nc.vector.quantize_mx(
                out=out_code[:, half, columns].bitcast(E4M3), scales=out_scale[:, half, columns], in_=tile[:]
            )
            nc.sync.dma_start(
                out=out_1[half, :, columns, :].rearrange("p m t -> p (m t)").bitcast(I32),
                in_=out_code[:, half, columns].bitcast(I32),
            )
            planes_left[half] -= 1
            if planes_left[half] == 0:
                for quadrant in range(4):
                    nc.sync.dma_start(
                        out=out_2[half, 4 * quadrant : 4 * quadrant + 4, :].bitcast(I32),
                        in_=out_scale[32 * quadrant : 32 * quadrant + 4, half, :].bitcast(I32),
                    )

        turn_input(0, 0)
        turn_input(0, 1)
        bias_bank = psum.tile([P, P], BF16, name="turn", bufs=4)
        nc.tensor.transpose(bias_bank[:], bias_rows[:], identity_bf16[:])
        group_input(0, 0, "scalar")
        group_input(0, 1, "vector")
        quantise_input(0, slice(0, GROUP // 2))
        quantise_input(0, slice(GROUP // 2, GROUP))
        turn_input(1, 0)
        turn_input(1, 1)
        project_x(0)
        project_x(1)
        group_input(1, 0, "scalar")
        group_input(1, 1, "vector")
        nc.scalar.copy(out=bias[:], in_=bias_bank[:, 0:BLOCKS])
        turn_input(2, 0)
        turn_input(2, 1)

        to_multiply, in_psum, rounded, to_turn, in_turn, to_quantise = [], [], [], [], [], []
        last_rows = [(LAST, 1, BANK * half, BANK) for half in (1, 0)]
        for i in range(PAIRS + 1):
            current = [2 * i, 2 * i + 1] if i < PAIRS else []

            if i > 0:
                first, second = 2 * i - 2, 2 * i - 1
                weigh(first)
                square(second)
            if i + 1 < 2 * GROUPS:
                quantise_input(i + 1, slice(0, GROUP))
            if i > 0:
                weigh(second)
                square(first)
            for c in current:
                tanh(c)
            if i + 2 < 2 * GROUPS:
                group_input(i + 2, 0, "scalar")
                group_input(i + 2, 1, "scalar")
            if i > 0:
                derive(second)
                derive(first)

            grouped_now = [(pair, half, group_result(bank, "scalar")) for pair, half, bank in in_turn]
            for rectangle, bank in in_psum:
                scale_and_store(rectangle, bank, "scalar")
            for pair, half, tile in to_quantise:
                quantise_and_store(pair, half, tile)
            to_quantise = grouped_now
            for rectangle in rounded:
                to_turn.extend(newly_complete(rectangle))
            if i > 0:
                quantise_pair(a_code, a_scale, weighted, first)
                quantise_pair(l_code, l_scale, derived, first)
            rounded = [rectangle for rectangle, bank in in_psum]
            for rectangle in rounded:
                round_result(rectangle, "gpsimd")

            for c in current:
                turn_psi(c)
            for c in current:
                project_f(c)
            for c in (2 * i + 2, 2 * i + 3):
                if c < len(CHUNKS):
                    project_x(c)
            if i + 3 < 2 * GROUPS:
                turn_input(i + 3, 0)
                turn_input(i + 3, 1)
            for lo, hi in SPANS[:-1]:
                if GROUPS * hi == 2 * i:
                    to_multiply.extend(new_rectangles(lo, hi))
            in_psum = [(rectangle, multiply(rectangle, "turn", 4)) for rectangle in to_multiply[:2]]
            to_multiply = to_multiply[2:]
            in_turn = [(pair, half, turn_result(pair, half, "turn", 4)) for pair, half in to_turn[:1]]
            to_turn = to_turn[1:]

        last_banks = [psum.tile([P, BANK], F32, name="z") for rectangle in last_rows]
        for g in range(GROUPS):
            for rectangle, bank in zip(last_rows, last_banks):
                add_group(bank[:], LAST, rectangle[2], g)
        last_columns = new_rectangles(LAST, BLOCKS)[:2]
        last_banks.extend([multiply(rectangle, "d", 2) for rectangle in last_columns])
        for pair, half, tile in to_quantise:
            quantise_and_store(pair, half, tile)
        for rectangle in rounded:
            to_turn.extend(newly_complete(rectangle))
        engines = [("vector", "gpsimd"), ("scalar", "vector"), ("vector", "vector"), ("scalar", "vector")]
        for rectangle, bank, (store_engine, round_engine) in zip(last_rows + last_columns, last_banks, engines):
            scale_and_store(rectangle, bank, store_engine)
            round_result(rectangle, round_engine)
            to_turn.extend(newly_complete(rectangle))

        for n, (pair, half) in enumerate(to_turn):
            bank = turn_result(pair, half, "d" if n % 2 else "turn", 2 if n % 2 else 4)
            tile = group_result(bank, "vector" if n % 2 else "scalar")
            if n > 0:
                quantise_and_store(*waiting)
            waiting = (pair, half, tile)
        quantise_and_store(*waiting)
